import numpy as np
import ml_dtypes


def mxq(x, axis, fmt="e4m3"):
    dtype, down = {"e4m3": (ml_dtypes.float8_e4m3fn, 7), "e5m2": (ml_dtypes.float8_e5m2, 14)}[fmt]
    v = np.moveaxis(np.asarray(x, np.float32).astype(ml_dtypes.bfloat16).astype(np.float64), axis, -1)
    blocks = v.reshape(v.shape[:-1] + (-1, 32))
    amax = np.abs(blocks).max(-1, keepdims=True)
    byte = np.maximum(np.where(amax > 0, np.frexp(amax)[1] - 1 + 127, 0) - down, 1)
    scale = np.exp2(byte - 127.0)
    codes = (blocks / scale).astype(np.float32).astype(dtype).astype(np.float64)
    return np.moveaxis((codes * scale).reshape(v.shape), -1, axis)


WIDE = False


def mx_kscale(k):
    if not WIDE:
        return np.ones(k)
    levels = np.array([10, -10, 5, -5, 0])
    if k % 512:
        return np.exp2(np.random.permutation(np.resize(levels, k // 32))).repeat(32)
    a = np.empty((k // 512, 16))
    for p in range(k // 512):
        a[p, :8] = np.random.permutation(np.resize(levels, 8))
        for g in range(8):
            far = levels[np.abs(levels - a[p, g]) >= 10]
            a[p, g + 8] = far[np.random.randint(len(far))]
    return np.exp2(a.ravel()).repeat(32)


BF16 = ml_dtypes.bfloat16


def bf(x):
    return np.asarray(x, np.float32).astype(BF16)


def f64(x):
    return np.asarray(x).astype(np.float64)


E2M1 = np.array([0.0, 0.5, 1.0, 1.5, 2.0, 3.0, 4.0, 6.0, -0.0, -0.5, -1.0, -1.5, -2.0, -3.0, -4.0, -6.0])


def pack_weight(w, fmt):
    k, n = w.shape
    w = f64(bf(w)).reshape(k // 32, 32, n)
    amax = np.abs(w).max(1)
    if fmt == "e4m3":
        byte = np.frexp(amax)[1] - 1 + 127 - 7
    else:
        mant, ex = np.frexp(amax / 6.0)
        byte = np.where(mant > 0.5, ex, ex - 1) + 127
    byte = np.clip(np.where(amax > 0, byte, 1), 1, 254)
    scaled = (w * np.exp2(127.0 - byte)[:, None, :]).reshape(k, n).astype(np.float32)
    by_word = np.ascontiguousarray(scaled.reshape(k // 512, 128, 4, n).transpose(0, 1, 3, 2))
    if fmt == "e4m3":
        words = by_word.astype(ml_dtypes.float8_e4m3fn).view(np.uint8)
    else:
        c = by_word.astype(ml_dtypes.float4_e2m1fn).view(np.uint8) & 0xF
        words = c[..., 0::2] | (c[..., 1::2] << 4)
    return np.ascontiguousarray(words), np.ascontiguousarray(byte.astype(np.uint8).reshape(k // 512, 16, n))


def unpack_weight(words, scales, fmt):
    g, p, n, _ = words.shape
    if fmt == "e4m3":
        vals = np.ascontiguousarray(words).view(ml_dtypes.float8_e4m3fn).astype(np.float64)
    else:
        nib = np.empty((g, p, n, 4), np.uint8)
        nib[..., 0::2] = words & 0xF
        nib[..., 1::2] = words >> 4
        vals = E2M1[nib]
    vals = vals * np.repeat(np.exp2(scales.astype(np.float64) - 127.0), 8, axis=1)[..., None]
    return vals.transpose(0, 1, 3, 2).reshape(g * 512, n)
def pack4(w):
    words, scales = pack_weight(w, "e2m1")
    return words.reshape(words.shape[0], 128, -1), scales


def unpack4(words, scales):
    return unpack_weight(words.reshape(words.shape[0], 128, -1, 2), scales, "e2m1")


def planes(Y):
    n, m = Y.shape
    b = f64(bf(Y)).reshape(n // 32, 32, m)
    amax = np.abs(b).max(1)
    byte = np.clip(np.where(amax > 0, np.frexp(amax)[1] - 1 + 127 - 7, 1), 1, 254)
    codes = (b * np.exp2(127.0 - byte)[:, None, :]).reshape(n, m).astype(np.float32).astype(ml_dtypes.float8_e4m3fn).view(np.uint8)
    words = codes.reshape(n // 512, 128, 4, m).transpose(0, 1, 3, 2)
    return np.ascontiguousarray(words), np.ascontiguousarray(byte.astype(np.uint8).reshape(n // 512, 16, m))


M, T, P, N = 2048, 512, 1024, 1536


def setup_inputs():
    noise = np.random.standard_normal
    s_now = mx_kscale(T)
    s_prev = mx_kscale(P)
    s_load = mx_kscale(T)
    e_now = 1.2 * noise((T, T)) / np.sqrt(T) - 0.8 * np.eye(T)
    e_prev = 1.2 * noise((P, T)) / np.sqrt(P)
    rates = 0.6 * noise((T, N)) / np.sqrt(T) * np.exp(0.7 * noise(N))[None, :]
    e_words, e_scales = pack4(e_prev / s_prev[:, None])
    r_words, r_scales = pack_weight(rates / s_load[:, None], "e4m3")
    return {
        "dlog_now": bf(0.3 * noise((M, T)) * s_now[None, :]),
        "dlog_prev": bf(0.3 * noise((M, P)) * s_prev[None, :]),
        "elast_now": bf(e_now / s_now[:, None]),
        "elast_prev_words": e_words,
        "elast_prev_scales": e_scales,
        "baseline": bf(np.exp(0.3 * noise((M, T))) * s_load[None, :]),
        "rate_words": r_words,
        "rate_scales": r_scales,
        "loss": bf(1 + 0.1 * noise(M)),
        "charge": bf(0.3 * noise(N)),
    }

def reference(dlog_now, dlog_prev, elast_now, elast_prev_words, elast_prev_scales, baseline, rate_words, rate_scales, loss, charge):
    E_prev = unpack4(elast_prev_words, elast_prev_scales)
    R = unpack_weight(rate_words, rate_scales, "e4m3")
    z = (mxq(f64(dlog_now), 1) @ mxq(f64(elast_now), 0)) + (mxq(f64(dlog_prev), 1) @ E_prev)
    load = f64(baseline) * np.exp(z)
    y = f64(loss)[:, None] * (mxq(load, 1) @ R) + f64(charge)[None, :]
    words, scales = planes(y.T)
    return y, words, scales

@@ -1,0 +1,341 @@
+from contextlib import ExitStack
+
+import concourse.mybir as mybir
+from concourse.masks import make_identity
+
+M, T, PREV, N = 2048, 512, 1024, 1536
+FLOPS = 2 * M * T * (T + PREV) + 2 * M * T * N
+
+F32 = mybir.dt.float32
+BF16 = mybir.dt.bfloat16
+U32 = mybir.dt.uint32
+I32 = mybir.dt.int32
+U8 = mybir.dt.uint8
+FP8X4 = mybir.dt.float8_e4m3fn_x4
+FP4X4 = mybir.dt.float4_e2m1fn_x4
+ACT = mybir.ActivationFunctionType
+ALU = mybir.AluOpType
+
+P = 128
+KP = 512
+TILES = M // P
+GROUPS = N // KP
+PAIR = 2
+EARLY_SCALE_TILES = 12
+AHEAD = 3
+
+
+def tile_cross_period_demand_settlement_k6_kernel(
+    tc, dlog_now, dlog_prev, elast_now, elast_prev_words, elast_prev_scales, baseline,
+    rate_words, rate_scales, loss, charge, out_0, out_1, out_2,
+):
+    nc = tc.nc
+    with ExitStack() as ctx:
+        keep = ctx.enter_context(tc.tile_pool(name="keep", bufs=1))
+        ring = ctx.enter_context(tc.tile_pool(name="ring", bufs=3))
+        loads = ctx.enter_context(tc.tile_pool(name="loads", bufs=AHEAD + 3))
+        results = ctx.enter_context(tc.tile_pool(name="results", bufs=5))
+        psum = ctx.enter_context(tc.psum_pool(name="psum", bufs=1))
+        ctx.enter_context(tc.manual_schedule())
+
+        ident = keep.tile([P, P], F32)
+        en_raw = keep.tile([P, 4 * T], BF16, align_bytes=64)
+        en_grouped = keep.tile([P, 4 * T], BF16, align_bytes=64)
+        en_codes = keep.tile([P, T], U32, align_bytes=64)
+        en_scales = keep.tile([P, T], U8, align_bytes=64)
+        ep_words = keep.tile([P, 2 * 2 * T], U8, align_bytes=64)
+        ep_scales = keep.tile([P, 2 * T], U8, align_bytes=64)
+        r_words = keep.tile([P, N], U32, align_bytes=64)
+        r_scales = keep.tile([P, N], U8, align_bytes=64)
+        loss_rows = keep.tile([P, P], BF16)
+        loss_rows32 = keep.tile([P, P], F32)
+        loss_cols = keep.tile([P, TILES + N // P], F32)
+        charge_all = keep.tile([P, N], F32)
+        warm = keep.tile([P, 8], F32)
+        scales_early = keep.tile([P, GROUPS * EARLY_SCALE_TILES * P], U8, align_bytes=64)
+        scales_late = keep.tile([P, GROUPS * (TILES - EARLY_SCALE_TILES) * P], U8, align_bytes=64)
+
+        x_now, x_prev, base, grouped, x_codes, x_scales = {}, {}, {}, {}, {}, {}
+        load_turned, l_codes, l_scales, z_banks, y_banks = {}, {}, {}, {}, {}
+        growth, load_bf, y32, y_bf, y_grouped, y_words = {}, {}, {}, {}, {}, {}
+
+        def rows(i):
+            return slice(i * P, (i + 1) * P)
+
+        def load_prices(i):
+            x_now[i] = loads.tile([P, T], BF16, name="x_now")
+            x_prev[i] = loads.tile([P, PREV], BF16, name="x_prev")
+            nc.sync.dma_start(out=x_now[i][:], in_=dlog_now[rows(i), :])
+            nc.sync.dma_start(out=x_prev[i][:], in_=dlog_prev[rows(i), :])
+
+        def load_baseline(i):
+            base[i] = loads.tile([P, T], BF16, name="base")
+            nc.sync.dma_start(out=base[i][:], in_=baseline[rows(i), :])
+
+        def load_scale_rows(queue, plane, src):
+            for q in range(4):
+                queue.dma_start(
+                    out=plane[32 * q : 32 * q + 4, :].bitcast(I32).rearrange("r (g n) -> r g n", g=src.shape[0]),
+                    in_=src[:, 4 * q : 4 * q + 4, :].bitcast(I32).rearrange("g r n -> r g n"),
+                )
+
+        def store_scale_rows(queues, plane, first, count):
+            for q in range(4):
+                queues[q % len(queues)].dma_start(
+                    out=out_2[:, 4 * q : 4 * q + 4, first * P : (first + count) * P].bitcast(I32).rearrange("g r m -> r g m"),
+                    in_=plane[32 * q : 32 * q + 4, :].bitcast(I32).rearrange("r (g m) -> r g m", g=GROUPS),
+                )
+
+        def copy_words(dst_words, bank, passes):
+            nc.scalar.copy(
+                out=dst_words.rearrange("p (g r u) -> p g r u", g=passes, u=2),
+                in_=bank[:, : passes * 256].rearrange("p (g u r) -> p g r u", g=passes, u=2),
+            )
+
+        def turn_prices(i):
+            grouped[i] = ring.tile([P, 3 * 256], F32, name="grouped", align_bytes=64)
+            bank_a = psum.tile([P, KP], F32, name="bank_a")
+            bank_b = psum.tile([P, KP], F32, name="bank_b")
+            now = x_now[i][:].bitcast(F32)
+            prev = x_prev[i][:].bitcast(F32)
+            for u in range(2):
+                nc.tensor.transpose(bank_a[:, u * P : (u + 1) * P], now[:, u:256:2], ident[:])
+            for u in range(2):
+                nc.tensor.transpose(bank_a[:, (2 + u) * P : (3 + u) * P], prev[:, u:256:2], ident[:])
+            for u in range(2):
+                nc.tensor.transpose(bank_b[:, u * P : (u + 1) * P], prev[:, 256 + u : 512 : 2], ident[:])
+            copy_words(grouped[i][:, 0:512], bank_a, 2)
+            copy_words(grouped[i][:, 512:768], bank_b, 1)
+
+        def quantise_prices(i):
+            x_codes[i] = ring.tile([P, 3 * P], U32, name="x_codes", align_bytes=64)
+            x_scales[i] = ring.tile([P, 3 * P], U8, name="x_scales", align_bytes=64)
+            for a, b in ((0, 2), (2, 3)):
+                nc.vector.quantize_mx(
+                    out=x_codes[i][:, a * P : b * P].bitcast(FP8X4),
+                    scales=x_scales[i][:, a * P : b * P],
+                    in_=grouped[i][:, a * 256 : b * 256].bitcast(BF16),
+                )
+
+        def turn_results(i_load, i_y):
+            turned = ring.tile([P, 4 * 256], F32, name="turned", align_bytes=64)
+            bank_d = psum.tile([P, KP], F32, name="bank_d")
+            if live(i_load):
+                load_turned[i_load] = turned
+                words = load_bf[i_load][:].bitcast(F32)
+                for u in range(2):
+                    nc.tensor.transpose(bank_d[:, (2 + u) * P : (3 + u) * P], words[:, u * P : (u + 1) * P], ident[:])
+            if live(i_y):
+                y_grouped[i_y] = turned
+                bank_c = psum.tile([P, KP], F32, name="bank_c")
+                for g in (2, 0, 1):
+                    words = y_bf[i_y, g][:].bitcast(F32)
+                    bank = bank_c if g < 2 else bank_d
+                    for u in range(2):
+                        at = (2 * (g % 2) + u) * P
+                        nc.tensor.transpose(bank[:, at : at + P], words[:, u * P : (u + 1) * P], ident[:])
+            if live(i_load) and live(i_y):
+                copy_words(turned[:, 512:1024], bank_d, 2)
+            elif live(i_load):
+                copy_words(turned[:, 768:1024], bank_d[:, 256:512], 1)
+            else:
+                copy_words(turned[:, 512:768], bank_d, 1)
+            if live(i_y):
+                copy_words(turned[:, 0:512], bank_c, 2)
+
+        def quantise_load(i):
+            l_codes[i] = ring.tile([P, P], U32, name="l_codes", align_bytes=64)
+            l_scales[i] = ring.tile([P, P], U8, name="l_scales", align_bytes=64)
+            nc.vector.quantize_mx(
+                out=l_codes[i][:].bitcast(FP8X4),
+                scales=l_scales[i][:],
+                in_=load_turned[i][:, 768:1024].bitcast(BF16),
+            )
+
+        def live(i):
+            return 0 <= i < TILES
+
+        def response(i):
+            bank_z = psum.tile([P, KP], F32, name="bank_z")
+            for g in range(3):
+                if g == 0:
+                    rhs, rhs_scale = en_codes[:].bitcast(FP8X4), en_scales[:]
+                else:
+                    rhs = ep_words[:, (g - 1) * 2 * T : g * 2 * T].bitcast(FP4X4)
+                    rhs_scale = ep_scales[:, (g - 1) * T : g * T]
+                nc.tensor.matmul_mx(
+                    out=bank_z[:],
+                    lhsT=x_codes[i][:, g * P : (g + 1) * P].bitcast(FP8X4),
+                    lhsT_scale=x_scales[i][:, g * P : (g + 1) * P],
+                    rhs=rhs,
+                    rhs_scale=rhs_scale,
+                    start=(g == 0),
+                    stop=(g == 2),
+                )
+            z_banks[i] = bank_z
+
+        def grow(i):
+            bank_z = z_banks[i]
+            growth[i] = ring.tile([P, T], F32, name="growth")
+            nc.scalar.activation(
+                out=growth[i][:].rearrange("m (u p e) -> m u p e", u=2, e=2),
+                in_=bank_z[:].rearrange("m (p u e) -> m u p e", u=2, e=2),
+                func=ACT.Exp,
+            )
+
+        def responded_load(i):
+            load_bf[i] = ring.tile([P, T], BF16, name="load_bf")
+            nc.vector.tensor_tensor(
+                out=load_bf[i][:].rearrange("m (u p e) -> m u p e", u=2, e=2),
+                in0=growth[i][:].rearrange("m (u p e) -> m u p e", u=2, e=2),
+                in1=base[i][:].rearrange("m (p u e) -> m u p e", u=2, e=2),
+                op=ALU.mult,
+            )
+
+        def settle(i):
+            y32[i] = results.tile([P, N], F32, name="y32")
+            banks = []
+            for g in range(GROUPS):
+                bank_y = psum.tile([P, KP], F32, name="bank_y%d" % g)
+                banks.append(bank_y)
+                nc.tensor.matmul_mx(
+                    out=bank_y[:],
+                    lhsT=l_codes[i][:].bitcast(FP8X4),
+                    lhsT_scale=l_scales[i][:],
+                    rhs=r_words[:, g * KP : (g + 1) * KP].bitcast(FP8X4),
+                    rhs_scale=r_scales[:, g * KP : (g + 1) * KP],
+                    start=True,
+                    stop=True,
+                )
+            y_banks[i] = banks
+
+        def finish_y(i):
+            banks = y_banks[i]
+            for g in range(GROUPS):
+                nc.vector.scalar_tensor_tensor(
+                    out=y32[i][:, g * KP : (g + 1) * KP],
+                    in0=banks[g][:],
+                    scalar=loss_cols[:, i : i + 1],
+                    in1=charge_all[:, g * KP : (g + 1) * KP],
+                    op0=ALU.mult,
+                    op1=ALU.add,
+                )
+            nc.sync.dma_start(out=out_0[rows(i), :], in_=y32[i][:])
+
+        def round_y(i, g, engine):
+            y_bf[i, g] = ring.tile([P, KP], BF16, name="y_bf%d" % g)
+            dst = y_bf[i, g][:].rearrange("m (u p e) -> m u p e", u=2, e=2)
+            src = y32[i][:, g * KP : (g + 1) * KP].rearrange("m (p u e) -> m u p e", u=2, e=2)
+            if engine == "scalar":
+                nc.scalar.copy(out=dst, in_=src)
+            elif engine == "vector":
+                nc.vector.tensor_copy(out=dst, in_=src)
+            else:
+                nc.gpsimd.tensor_scalar(out=dst, in0=src, scalar1=1.0, scalar2=0.0, op0=ALU.mult, op1=ALU.add)
+
+        def quantise_y(i):
+            pair, j = divmod(i, PAIR)
+            if j == 0:
+                y_words[pair] = ring.tile([P, GROUPS * PAIR * P], U32, name="y_words", align_bytes=64)
+            if i < EARLY_SCALE_TILES:
+                plane, at, count = scales_early, i, EARLY_SCALE_TILES
+            else:
+                plane, at, count = scales_late, i - EARLY_SCALE_TILES, TILES - EARLY_SCALE_TILES
+            for g in range(GROUPS):
+                nc.vector.quantize_mx(
+                    out=y_words[pair][:, (g * PAIR + j) * P : (g * PAIR + j + 1) * P].bitcast(FP8X4),
+                    scales=plane[:, (g * count + at) * P : (g * count + at + 1) * P],
+                    in_=y_grouped[i][:, g * 256 : (g + 1) * 256].bitcast(BF16),
+                )
+            if j == PAIR - 1:
+                words_out = out_1.rearrange("g p m t -> p g (m t)")
+                nc.sync.dma_start(
+                    out=words_out[:, :, pair * PAIR * P * 4 : (pair + 1) * PAIR * P * 4].bitcast(I32),
+                    in_=y_words[pair][:].bitcast(I32).rearrange("p (g m) -> p g m", g=GROUPS),
+                )
+            if i == EARLY_SCALE_TILES - 1:
+                store_scale_rows([nc.sync], scales_early, 0, EARLY_SCALE_TILES)
+            if i == TILES - 1:
+                store_scale_rows([nc.scalar, nc.sync], scales_late, EARLY_SCALE_TILES, TILES - EARLY_SCALE_TILES)
+
+        nc.vector.memset(loss_rows[:], 0.0)
+        nc.vector.memset(ep_scales[:].bitcast(I32), 0)
+        nc.vector.memset(warm[:], 0.0)
+        nc.scalar.activation(out=warm[:, 4:5], in_=warm[:, 0:1], func=ACT.Exp)
+        nc.vector.memset(r_scales[:].bitcast(I32), 0)
+        nc.gpsimd.dma_start(out=loss_rows[0:TILES, :], in_=loss.rearrange("(i p) -> i p", p=P))
+        nc.gpsimd.dma_start(out=loss_rows[TILES : TILES + N // P, :], in_=charge.rearrange("(c p) -> c p", p=P))
+        make_identity(nc, ident[:])
+        nc.sync.dma_start(out=en_raw[:], in_=elast_now.rearrange("(p j) n -> p (j n)", j=4))
+        load_prices(0)
+        load_scale_rows(nc.sync, ep_scales, elast_prev_scales)
+        nc.sync.dma_start(
+            out=ep_words[:].bitcast(I32).rearrange("p (g n) -> p g n", g=2),
+            in_=elast_prev_words.bitcast(I32).rearrange("g p n -> p g n"),
+        )
+        load_scale_rows(nc.gpsimd, r_scales, rate_scales)
+        load_prices(1)
+        load_baseline(0)
+        load_prices(2)
+        nc.sync.dma_start(
+            out=r_words[:].bitcast(I32),
+            in_=rate_words[0].rearrange("p n t -> p (n t)").bitcast(I32),
+        )
+        load_baseline(1)
+        nc.vector.tensor_copy(
+            out=en_grouped[:].rearrange("p (c i j) -> p c j i", i=4, j=4),
+            in_=en_raw[:].rearrange("p (j c i) -> p c j i", j=4, i=4),
+        )
+        nc.vector.quantize_mx(out=en_codes[:].bitcast(FP8X4), scales=en_scales[:], in_=en_grouped[:])
+
+        def spread_loss():
+            nc.scalar.copy(out=loss_rows32[:], in_=loss_rows[:])
+            bank_loss = psum.tile([P, KP], F32, name="bank_c")
+            nc.tensor.transpose(bank_loss[:, 0:P], loss_rows32[:], ident[:])
+            nc.scalar.copy(out=loss_cols[:], in_=bank_loss[:, 0 : TILES + N // P])
+
+        def spread_charge():
+            for g in range(GROUPS):
+                bank_charge = psum.tile([P, KP], F32, name="bank_y%d" % g)
+                for c in range(4):
+                    col = TILES + 4 * g + c
+                    nc.tensor.transpose(
+                        bank_charge[:, c * P : (c + 1) * P], loss_cols[:, col : col + 1].to_broadcast([P, P]), ident[:]
+                    )
+                nc.vector.tensor_copy(out=charge_all[:, g * KP : (g + 1) * KP], in_=bank_charge[:])
+
+        for s in range(TILES + 5):
+            if live(s + AHEAD):
+                load_prices(s + AHEAD)
+            if live(s + 2):
+                load_baseline(s + 2)
+            if live(s - 1):
+                grow(s - 1)
+            if live(s - 3):
+                round_y(s - 3, 1, "vector")
+            if live(s - 2):
+                quantise_load(s - 2)
+            if live(s - 5):
+                quantise_y(s - 5)
+            if live(s - 0):
+                turn_prices(s - 0)
+            if live(s - 1):
+                responded_load(s - 1)
+            if live(s - 0):
+                quantise_prices(s - 0)
+            if s == 0:
+                spread_loss()
+            if live(s - 2):
+                settle(s - 2)
+            if live(s - 3):
+                round_y(s - 3, 2, "scalar")
+            if live(s - 3):
+                round_y(s - 3, 0, "scalar")
+            if live(s - 2):
+                finish_y(s - 2)
+            if live(s - 1) or live(s - 4):
+                turn_results(s - 1, s - 4)
+            if live(s - 0):
+                response(s - 0)
+            if s == 0:
+                spread_charge()

@@ -21,8 +21,8 @@ KP = 512
 TILES = M // P
 GROUPS = N // KP
 PAIR = 2
-EARLY_SCALE_TILES = 12
-AHEAD = 3
+EARLY_SCALE_TILES = 10
+AHEAD = 4
 
 
 def tile_cross_period_demand_settlement_k6_kernel(
@@ -56,7 +56,7 @@ def tile_cross_period_demand_settlement_k6_kernel(
         scales_late = keep.tile([P, GROUPS * (TILES - EARLY_SCALE_TILES) * P], U8, align_bytes=64)
 
         x_now, x_prev, base, grouped, x_codes, x_scales = {}, {}, {}, {}, {}, {}
-        load_turned, l_codes, l_scales, z_banks, y_banks = {}, {}, {}, {}, {}
+        y_banks = {}
         growth, load_bf, y32, y_bf, y_grouped, y_words = {}, {}, {}, {}, {}, {}
 
         def rows(i):
@@ -92,72 +92,51 @@ def tile_cross_period_demand_settlement_k6_kernel(
                 in_=bank[:, : passes * 256].rearrange("p (g u r) -> p g r u", g=passes, u=2),
             )
 
-        def turn_prices(i):
-            grouped[i] = ring.tile([P, 3 * 256], F32, name="grouped", align_bytes=64)
-            bank_a = psum.tile([P, KP], F32, name="bank_a")
+        def turn_front(s):
+            grouped[s] = ring.tile([P, 4 * 256], F32, name="grouped", align_bytes=64)
             bank_b = psum.tile([P, KP], F32, name="bank_b")
-            now = x_now[i][:].bitcast(F32)
-            prev = x_prev[i][:].bitcast(F32)
-            for u in range(2):
-                nc.tensor.transpose(bank_a[:, u * P : (u + 1) * P], now[:, u:256:2], ident[:])
-            for u in range(2):
-                nc.tensor.transpose(bank_a[:, (2 + u) * P : (3 + u) * P], prev[:, u:256:2], ident[:])
-            for u in range(2):
-                nc.tensor.transpose(bank_b[:, u * P : (u + 1) * P], prev[:, 256 + u : 512 : 2], ident[:])
-            copy_words(grouped[i][:, 0:512], bank_a, 2)
-            copy_words(grouped[i][:, 512:768], bank_b, 1)
-
-        def quantise_prices(i):
-            x_codes[i] = ring.tile([P, 3 * P], U32, name="x_codes", align_bytes=64)
-            x_scales[i] = ring.tile([P, 3 * P], U8, name="x_scales", align_bytes=64)
-            for a, b in ((0, 2), (2, 3)):
-                nc.vector.quantize_mx(
-                    out=x_codes[i][:, a * P : b * P].bitcast(FP8X4),
-                    scales=x_scales[i][:, a * P : b * P],
-                    in_=grouped[i][:, a * 256 : b * 256].bitcast(BF16),
-                )
-
-        def turn_results(i_load, i_y):
-            turned = ring.tile([P, 4 * 256], F32, name="turned", align_bytes=64)
-            bank_d = psum.tile([P, KP], F32, name="bank_d")
-            if live(i_load):
-                load_turned[i_load] = turned
-                words = load_bf[i_load][:].bitcast(F32)
+            if s < TILES:
+                bank_a = psum.tile([P, KP], F32, name="bank_a")
+                now = x_now[s][:].bitcast(F32)
+                prev = x_prev[s][:].bitcast(F32)
                 for u in range(2):
-                    nc.tensor.transpose(bank_d[:, (2 + u) * P : (3 + u) * P], words[:, u * P : (u + 1) * P], ident[:])
-            if live(i_y):
-                y_grouped[i_y] = turned
-                bank_c = psum.tile([P, KP], F32, name="bank_c")
-                for g in (2, 0, 1):
-                    words = y_bf[i_y, g][:].bitcast(F32)
-                    bank = bank_c if g < 2 else bank_d
-                    for u in range(2):
-                        at = (2 * (g % 2) + u) * P
-                        nc.tensor.transpose(bank[:, at : at + P], words[:, u * P : (u + 1) * P], ident[:])
-            if live(i_load) and live(i_y):
-                copy_words(turned[:, 512:1024], bank_d, 2)
-            elif live(i_load):
-                copy_words(turned[:, 768:1024], bank_d[:, 256:512], 1)
+                    nc.tensor.transpose(bank_a[:, u * P : (u + 1) * P], now[:, u:256:2], ident[:])
+                for u in range(2):
+                    nc.tensor.transpose(bank_a[:, (2 + u) * P : (3 + u) * P], prev[:, u:256:2], ident[:])
+                for u in range(2):
+                    nc.tensor.transpose(bank_b[:, u * P : (u + 1) * P], prev[:, 256 + u : 512 : 2], ident[:])
+            if s >= 3:
+                words = load_bf[s - 3][:].bitcast(F32)
+                for u in range(2):
+                    nc.tensor.transpose(bank_b[:, (2 + u) * P : (3 + u) * P], words[:, u * P : (u + 1) * P], ident[:])
+            if s < TILES:
+                copy_words(grouped[s][:, 0:512], bank_a, 2)
+            if s < 3:
+                copy_words(grouped[s][:, 512:768], bank_b, 1)
+            elif s < TILES:
+                copy_words(grouped[s][:, 512:1024], bank_b, 2)
             else:
-                copy_words(turned[:, 512:768], bank_d, 1)
-            if live(i_y):
-                copy_words(turned[:, 0:512], bank_c, 2)
+                copy_words(grouped[s][:, 768:1024], bank_b[:, 256:512], 1)
 
-        def quantise_load(i):
-            l_codes[i] = ring.tile([P, P], U32, name="l_codes", align_bytes=64)
-            l_scales[i] = ring.tile([P, P], U8, name="l_scales", align_bytes=64)
-            nc.vector.quantize_mx(
-                out=l_codes[i][:].bitcast(FP8X4),
-                scales=l_scales[i][:],
-                in_=load_turned[i][:, 768:1024].bitcast(BF16),
-            )
-
-        def live(i):
-            return 0 <= i < TILES
+        def quantise_front(s):
+            x_codes[s] = ring.tile([P, 4 * P], U32, name="x_codes", align_bytes=64)
+            x_scales[s] = ring.tile([P, 4 * P], U8, name="x_scales", align_bytes=64)
+            if s < 3:
+                spans = [(0, 2), (2, 3)]
+            elif s < TILES:
+                spans = [(0, 4)]
+            else:
+                spans = [(3, 4)]
+            for a, b in spans:
+                nc.vector.quantize_mx(
+                    out=x_codes[s][:, a * P : b * P].bitcast(FP8X4),
+                    scales=x_scales[s][:, a * P : b * P],
+                    in_=grouped[s][:, a * 256 : b * 256].bitcast(BF16),
+                )
 
         def response(i):
             bank_z = psum.tile([P, KP], F32, name="bank_z")
-            for g in range(3):
+            for g in (1, 2, 0):
                 if g == 0:
                     rhs, rhs_scale = en_codes[:].bitcast(FP8X4), en_scales[:]
                 else:
@@ -169,13 +148,9 @@ def tile_cross_period_demand_settlement_k6_kernel(
                     lhsT_scale=x_scales[i][:, g * P : (g + 1) * P],
                     rhs=rhs,
                     rhs_scale=rhs_scale,
-                    start=(g == 0),
-                    stop=(g == 2),
+                    start=(g == 1),
+                    stop=(g == 0),
                 )
-            z_banks[i] = bank_z
-
-        def grow(i):
-            bank_z = z_banks[i]
             growth[i] = ring.tile([P, T], F32, name="growth")
             nc.scalar.activation(
                 out=growth[i][:].rearrange("m (u p e) -> m u p e", u=2, e=2),
@@ -184,8 +159,8 @@ def tile_cross_period_demand_settlement_k6_kernel(
             )
 
         def responded_load(i):
-            load_bf[i] = ring.tile([P, T], BF16, name="load_bf")
-            nc.vector.tensor_tensor(
+            load_bf[i] = ring.tile([P, T], BF16, name="load_bf", bufs=4)
+            nc.gpsimd.tensor_tensor(
                 out=load_bf[i][:].rearrange("m (u p e) -> m u p e", u=2, e=2),
                 in0=growth[i][:].rearrange("m (u p e) -> m u p e", u=2, e=2),
                 in1=base[i][:].rearrange("m (p u e) -> m u p e", u=2, e=2),
@@ -200,8 +175,8 @@ def tile_cross_period_demand_settlement_k6_kernel(
                 banks.append(bank_y)
                 nc.tensor.matmul_mx(
                     out=bank_y[:],
-                    lhsT=l_codes[i][:].bitcast(FP8X4),
-                    lhsT_scale=l_scales[i][:],
+                    lhsT=x_codes[i + 3][:, 3 * P : 4 * P].bitcast(FP8X4),
+                    lhsT_scale=x_scales[i + 3][:, 3 * P : 4 * P],
                     rhs=r_words[:, g * KP : (g + 1) * KP].bitcast(FP8X4),
                     rhs_scale=r_scales[:, g * KP : (g + 1) * KP],
                     start=True,
@@ -211,6 +186,7 @@ def tile_cross_period_demand_settlement_k6_kernel(
 
         def finish_y(i):
             banks = y_banks[i]
+            last = i >= 12
             for g in range(GROUPS):
                 nc.vector.scalar_tensor_tensor(
                     out=y32[i][:, g * KP : (g + 1) * KP],
@@ -220,7 +196,11 @@ def tile_cross_period_demand_settlement_k6_kernel(
                     op0=ALU.mult,
                     op1=ALU.add,
                 )
-            nc.sync.dma_start(out=out_0[rows(i), :], in_=y32[i][:])
+                if last:
+                    cols = slice(g * KP, (g + 1) * KP)
+                    nc.sync.dma_start(out=out_0[rows(i), cols], in_=y32[i][:, cols])
+            if not last:
+                nc.sync.dma_start(out=out_0[rows(i), :], in_=y32[i][:])
 
         def round_y(i, g, engine):
             y_bf[i, g] = ring.tile([P, KP], BF16, name="y_bf%d" % g)
@@ -233,24 +213,39 @@ def tile_cross_period_demand_settlement_k6_kernel(
             else:
                 nc.gpsimd.tensor_scalar(out=dst, in0=src, scalar1=1.0, scalar2=0.0, op0=ALU.mult, op1=ALU.add)
 
+        def turn_y(i, first="bank_c", second="bank_d"):
+            bank_c = psum.tile([P, KP], F32, name=first)
+            bank_d = psum.tile([P, KP], F32, name=second)
+            for g in range(GROUPS):
+                words = y_bf[i, g][:].bitcast(F32)
+                bank = bank_c if g < 2 else bank_d
+                for u in range(2):
+                    at = (2 * (g % 2) + u) * P
+                    nc.tensor.transpose(bank[:, at : at + P], words[:, u * P : (u + 1) * P], ident[:])
+            y_grouped[i] = ring.tile([P, GROUPS * 256], F32, name="y_grouped", align_bytes=64)
+            copy_words(y_grouped[i][:, 0:512], bank_c, 2)
+            copy_words(y_grouped[i][:, 512:768], bank_d, 1)
+
         def quantise_y(i):
-            pair, j = divmod(i, PAIR)
+            width = PAIR
+            j = i % width
+            pair = i - j
             if j == 0:
-                y_words[pair] = ring.tile([P, GROUPS * PAIR * P], U32, name="y_words", align_bytes=64)
+                y_words[pair] = ring.tile([P, GROUPS * width * P], U32, name="y_words", align_bytes=64)
             if i < EARLY_SCALE_TILES:
                 plane, at, count = scales_early, i, EARLY_SCALE_TILES
             else:
                 plane, at, count = scales_late, i - EARLY_SCALE_TILES, TILES - EARLY_SCALE_TILES
             for g in range(GROUPS):
                 nc.vector.quantize_mx(
-                    out=y_words[pair][:, (g * PAIR + j) * P : (g * PAIR + j + 1) * P].bitcast(FP8X4),
+                    out=y_words[pair][:, (g * width + j) * P : (g * width + j + 1) * P].bitcast(FP8X4),
                     scales=plane[:, (g * count + at) * P : (g * count + at + 1) * P],
                     in_=y_grouped[i][:, g * 256 : (g + 1) * 256].bitcast(BF16),
                 )
-            if j == PAIR - 1:
+            if j == width - 1:
                 words_out = out_1.rearrange("g p m t -> p g (m t)")
                 nc.sync.dma_start(
-                    out=words_out[:, :, pair * PAIR * P * 4 : (pair + 1) * PAIR * P * 4].bitcast(I32),
+                    out=words_out[:, :, pair * P * 4 : (pair + width) * P * 4].bitcast(I32),
                     in_=y_words[pair][:].bitcast(I32).rearrange("p (g m) -> p g m", g=GROUPS),
                 )
             if i == EARLY_SCALE_TILES - 1:
@@ -263,11 +258,11 @@ def tile_cross_period_demand_settlement_k6_kernel(
         nc.vector.memset(warm[:], 0.0)
         nc.scalar.activation(out=warm[:, 4:5], in_=warm[:, 0:1], func=ACT.Exp)
         nc.vector.memset(r_scales[:].bitcast(I32), 0)
-        nc.gpsimd.dma_start(out=loss_rows[0:TILES, :], in_=loss.rearrange("(i p) -> i p", p=P))
-        nc.gpsimd.dma_start(out=loss_rows[TILES : TILES + N // P, :], in_=charge.rearrange("(c p) -> c p", p=P))
         make_identity(nc, ident[:])
-        nc.sync.dma_start(out=en_raw[:], in_=elast_now.rearrange("(p j) n -> p (j n)", j=4))
         load_prices(0)
+        nc.sync.dma_start(out=loss_rows[0:TILES, :], in_=loss.rearrange("(i p) -> i p", p=P))
+        nc.sync.dma_start(out=loss_rows[TILES : TILES + N // P, :], in_=charge.rearrange("(c p) -> c p", p=P))
+        nc.sync.dma_start(out=en_raw[:], in_=elast_now.rearrange("(p j) n -> p (j n)", j=4))
         load_scale_rows(nc.sync, ep_scales, elast_prev_scales)
         nc.sync.dma_start(
             out=ep_words[:].bitcast(I32).rearrange("p (g n) -> p g n", g=2),
@@ -275,18 +270,25 @@ def tile_cross_period_demand_settlement_k6_kernel(
         )
         load_scale_rows(nc.gpsimd, r_scales, rate_scales)
         load_prices(1)
-        load_baseline(0)
         load_prices(2)
+        load_baseline(0)
+        load_prices(3)
         nc.sync.dma_start(
             out=r_words[:].bitcast(I32),
             in_=rate_words[0].rearrange("p n t -> p (n t)").bitcast(I32),
         )
+        load_prices(4)
         load_baseline(1)
-        nc.vector.tensor_copy(
-            out=en_grouped[:].rearrange("p (c i j) -> p c j i", i=4, j=4),
-            in_=en_raw[:].rearrange("p (j c i) -> p c j i", j=4, i=4),
-        )
-        nc.vector.quantize_mx(out=en_codes[:].bitcast(FP8X4), scales=en_scales[:], in_=en_grouped[:])
+
+        def quantise_elasticities():
+            dst = en_grouped[:].rearrange("p (c i j) -> p c j i", i=4, j=4)
+            src = en_raw[:].rearrange("p (j c i) -> p c j i", j=4, i=4)
+            nc.vector.tensor_copy(out=dst[:, 0:88], in_=src[:, 0:88])
+            nc.scalar.copy(out=dst[:, 88:128], in_=src[:, 88:128])
+            nc.vector.quantize_mx(out=en_codes[:].bitcast(FP8X4), scales=en_scales[:], in_=en_grouped[:])
+
+        def live(i):
+            return 0 <= i < TILES
 
         def spread_loss():
             nc.scalar.copy(out=loss_rows32[:], in_=loss_rows[:])
@@ -304,38 +306,68 @@ def tile_cross_period_demand_settlement_k6_kernel(
                     )
                 nc.vector.tensor_copy(out=charge_all[:, g * KP : (g + 1) * KP], in_=bank_charge[:])
 
-        for s in range(TILES + 5):
+        spread_loss()
+        turn_front(0)
+        quantise_front(0)
+        quantise_elasticities()
+        spread_charge()
+        for s in range(1, TILES + 1):
             if live(s + AHEAD):
                 load_prices(s + AHEAD)
-            if live(s + 2):
-                load_baseline(s + 2)
-            if live(s - 1):
-                grow(s - 1)
-            if live(s - 3):
-                round_y(s - 3, 1, "vector")
-            if live(s - 2):
-                quantise_load(s - 2)
+            if live(s + 1):
+                load_baseline(s + 1)
             if live(s - 5):
-                quantise_y(s - 5)
-            if live(s - 0):
-                turn_prices(s - 0)
+                round_y(s - 5, 0, "vector")
+            if live(s - 5):
+                round_y(s - 5, 1, "vector")
+            if s < TILES + 3:
+                turn_front(s)
+            if s < TILES + 3:
+                quantise_front(s)
+            if live(s - 7):
+                quantise_y(s - 7)
+            if live(s - 1):
+                response(s - 1)
             if live(s - 1):
                 responded_load(s - 1)
-            if live(s - 0):
-                quantise_prices(s - 0)
-            if s == 0:
-                spread_loss()
-            if live(s - 2):
-                settle(s - 2)
-            if live(s - 3):
-                round_y(s - 3, 2, "scalar")
-            if live(s - 3):
-                round_y(s - 3, 0, "scalar")
-            if live(s - 2):
-                finish_y(s - 2)
-            if live(s - 1) or live(s - 4):
-                turn_results(s - 1, s - 4)
-            if live(s - 0):
-                response(s - 0)
-            if s == 0:
-                spread_charge()
+            if live(s - 6):
+                turn_y(s - 6)
+            if live(s - 5):
+                round_y(s - 5, 2, "scalar")
+            if live(s - 4):
+                settle(s - 4)
+            if live(s - 4):
+                finish_y(s - 4)
+        round_y(12, 0, "scalar")
+        turn_front(17)
+        round_y(12, 1, "scalar")
+        quantise_front(17)
+        quantise_y(10)
+        round_y(12, 2, "gpsimd")
+        turn_y(11)
+        settle(13)
+        finish_y(13)
+        turn_front(18)
+        round_y(13, 0, "gpsimd")
+        quantise_front(18)
+        quantise_y(11)
+        turn_y(12, "bank_a", "bank_z")
+        round_y(13, 1, "scalar")
+        round_y(13, 2, "scalar")
+        quantise_y(12)
+        settle(14)
+        finish_y(14)
+        turn_y(13)
+        round_y(14, 0, "gpsimd")
+        round_y(14, 1, "gpsimd")
+        settle(15)
+        round_y(14, 2, "scalar")
+        finish_y(15)
+        round_y(15, 0, "gpsimd")
+        round_y(15, 1, "scalar")
+        quantise_y(13)
+        turn_y(14, "bank_a", "bank_z")
+        round_y(15, 2, "vector")
+        turn_y(15)
+        quantise_y(14)
+        quantise_y(15)

@@ -56,7 +56,7 @@ def tile_cross_period_demand_settlement_k6_kernel(
         scales_late = keep.tile([P, GROUPS * (TILES - EARLY_SCALE_TILES) * P], U8, align_bytes=64)
 
         x_now, x_prev, base, grouped, x_codes, x_scales = {}, {}, {}, {}, {}, {}
-        y_banks = {}
+        y_banks, x_sorted = {}, {}
         growth, load_bf, y32, y_bf, y_grouped, y_words = {}, {}, {}, {}, {}, {}
 
         def rows(i):
@@ -92,19 +92,34 @@ def tile_cross_period_demand_settlement_k6_kernel(
                 in_=bank[:, : passes * 256].rearrange("p (g u r) -> p g r u", g=passes, u=2),
             )
 
+        def sort_words(i, g, engine):
+            source = x_now[i][:].bitcast(F32) if g == 0 else x_prev[i][:].bitcast(F32)[:, (g - 1) * 256 : g * 256]
+            x_sorted[i, g] = ring.tile([P, 256], F32, name="x_sorted%d" % g, bufs=4)
+            dst = x_sorted[i, g][:].rearrange("m (u p) -> m u p", u=2)
+            src = source.rearrange("m (p u) -> m u p", u=2)
+            if engine == "scalar":
+                nc.scalar.copy(out=dst, in_=src)
+            else:
+                nc.vector.tensor_copy(out=dst, in_=src)
+
+        def price_words(i, g, u):
+            if (i, g) in x_sorted:
+                return x_sorted[i, g][:, u * P : (u + 1) * P]
+            if g == 0:
+                return x_now[i][:].bitcast(F32)[:, u:256:2]
+            return x_prev[i][:].bitcast(F32)[:, (g - 1) * 256 + u : g * 256 : 2]
+
         def turn_front(s):
             grouped[s] = ring.tile([P, 4 * 256], F32, name="grouped", align_bytes=64)
             bank_b = psum.tile([P, KP], F32, name="bank_b")
             if s < TILES:
                 bank_a = psum.tile([P, KP], F32, name="bank_a")
-                now = x_now[s][:].bitcast(F32)
-                prev = x_prev[s][:].bitcast(F32)
                 for u in range(2):
-                    nc.tensor.transpose(bank_a[:, u * P : (u + 1) * P], now[:, u:256:2], ident[:])
+                    nc.tensor.transpose(bank_a[:, u * P : (u + 1) * P], price_words(s, 0, u), ident[:])
                 for u in range(2):
-                    nc.tensor.transpose(bank_a[:, (2 + u) * P : (3 + u) * P], prev[:, u:256:2], ident[:])
+                    nc.tensor.transpose(bank_a[:, (2 + u) * P : (3 + u) * P], price_words(s, 1, u), ident[:])
                 for u in range(2):
-                    nc.tensor.transpose(bank_b[:, u * P : (u + 1) * P], prev[:, 256 + u : 512 : 2], ident[:])
+                    nc.tensor.transpose(bank_b[:, u * P : (u + 1) * P], price_words(s, 2, u), ident[:])
             if s >= 3:
                 words = load_bf[s - 3][:].bitcast(F32)
                 for u in range(2):
@@ -159,7 +174,7 @@ def tile_cross_period_demand_settlement_k6_kernel(
             )
 
         def responded_load(i):
-            load_bf[i] = ring.tile([P, T], BF16, name="load_bf", bufs=4)
+            load_bf[i] = ring.tile([P, T], BF16, name="load_bf", tag="handover", align_bytes=64)
             nc.gpsimd.tensor_tensor(
                 out=load_bf[i][:].rearrange("m (u p e) -> m u p e", u=2, e=2),
                 in0=growth[i][:].rearrange("m (u p e) -> m u p e", u=2, e=2),
@@ -213,6 +228,14 @@ def tile_cross_period_demand_settlement_k6_kernel(
             else:
                 nc.gpsimd.tensor_scalar(out=dst, in0=src, scalar1=1.0, scalar2=0.0, op0=ALU.mult, op1=ALU.add)
 
+        def round_y_pair(i):
+            pair_bf = ring.tile([P, 2 * KP], BF16, name="y_bf_pair")
+            y_bf[i, 0], y_bf[i, 1] = pair_bf[:, 0:KP], pair_bf[:, KP : 2 * KP]
+            nc.vector.tensor_copy(
+                out=pair_bf[:].rearrange("m (g u p e) -> m g u p e", g=2, u=2, e=2),
+                in_=y32[i][:, 0 : 2 * KP].rearrange("m (g p u e) -> m g u p e", g=2, u=2, e=2),
+            )
+
         def turn_y(i, first="bank_c", second="bank_d"):
             bank_c = psum.tile([P, KP], F32, name=first)
             bank_d = psum.tile([P, KP], F32, name=second)
@@ -222,7 +245,7 @@ def tile_cross_period_demand_settlement_k6_kernel(
                 for u in range(2):
                     at = (2 * (g % 2) + u) * P
                     nc.tensor.transpose(bank[:, at : at + P], words[:, u * P : (u + 1) * P], ident[:])
-            y_grouped[i] = ring.tile([P, GROUPS * 256], F32, name="y_grouped", align_bytes=64)
+            y_grouped[i] = ring.tile([P, GROUPS * 256], F32, name="y_grouped", tag="handover", align_bytes=64)
             copy_words(y_grouped[i][:, 0:512], bank_c, 2)
             copy_words(y_grouped[i][:, 512:768], bank_d, 1)
 
@@ -311,17 +334,21 @@ def tile_cross_period_demand_settlement_k6_kernel(
         quantise_front(0)
         quantise_elasticities()
         spread_charge()
+        sort_words(2, 0, "vector")
+        sort_words(2, 1, "scalar")
         for s in range(1, TILES + 1):
             if live(s + AHEAD):
                 load_prices(s + AHEAD)
             if live(s + 1):
                 load_baseline(s + 1)
             if live(s - 5):
-                round_y(s - 5, 0, "vector")
-            if live(s - 5):
-                round_y(s - 5, 1, "vector")
+                round_y_pair(s - 5)
+            if live(s + 2):
+                sort_words(s + 2, 0, "vector")
             if s < TILES + 3:
                 turn_front(s)
+            if live(s - 6):
+                turn_y(s - 6)
             if s < TILES + 3:
                 quantise_front(s)
             if live(s - 7):
@@ -330,10 +357,10 @@ def tile_cross_period_demand_settlement_k6_kernel(
                 response(s - 1)
             if live(s - 1):
                 responded_load(s - 1)
-            if live(s - 6):
-                turn_y(s - 6)
             if live(s - 5):
                 round_y(s - 5, 2, "scalar")
+            if live(s + 2):
+                sort_words(s + 2, 1, "scalar")
             if live(s - 4):
                 settle(s - 4)
             if live(s - 4):

@@ -17,12 +17,26 @@ ACT = mybir.ActivationFunctionType
 ALU = mybir.AluOpType
 
 P = 128
-KP = 512
+GROUP = 512
+PAIRS = GROUP // 2
 TILES = M // P
-GROUPS = N // KP
-PAIR = 2
+Y_GROUPS = N // GROUP
+CHARGE_ROWS = N // P
+
+LAG_Z = 1
+LAG_LOAD = 3
+LAG_Y = 4
+LAG_ROUND = 5
+LAG_TURN_Y = 6
+LAG_PLANES = 7
+LOAD_AHEAD = 4
+SORT_AHEAD = 2
+
+SORTED_GROUP = 1
+ELAST_ON_VECTOR = 88
+WORD_TILES = 2
 EARLY_SCALE_TILES = 10
-AHEAD = 4
+FIRST_SPLIT_STORE = 12
 
 
 def tile_cross_period_demand_settlement_k6_kernel(
@@ -33,34 +47,42 @@ def tile_cross_period_demand_settlement_k6_kernel(
     with ExitStack() as ctx:
         keep = ctx.enter_context(tc.tile_pool(name="keep", bufs=1))
         ring = ctx.enter_context(tc.tile_pool(name="ring", bufs=3))
-        loads = ctx.enter_context(tc.tile_pool(name="loads", bufs=AHEAD + 3))
+        loads = ctx.enter_context(tc.tile_pool(name="loads", bufs=LOAD_AHEAD + 3))
         results = ctx.enter_context(tc.tile_pool(name="results", bufs=5))
         psum = ctx.enter_context(tc.psum_pool(name="psum", bufs=1))
         ctx.enter_context(tc.manual_schedule())
 
         ident = keep.tile([P, P], F32)
-        en_raw = keep.tile([P, 4 * T], BF16, align_bytes=64)
-        en_grouped = keep.tile([P, 4 * T], BF16, align_bytes=64)
-        en_codes = keep.tile([P, T], U32, align_bytes=64)
-        en_scales = keep.tile([P, T], U8, align_bytes=64)
-        ep_words = keep.tile([P, 2 * 2 * T], U8, align_bytes=64)
-        ep_scales = keep.tile([P, 2 * T], U8, align_bytes=64)
+        elast_raw = keep.tile([P, 4 * T], BF16, align_bytes=64)
+        elast_grouped = keep.tile([P, 4 * T], BF16, align_bytes=64)
+        elast_codes = keep.tile([P, T], U32, align_bytes=64)
+        elast_scales = keep.tile([P, T], U8, align_bytes=64)
+        eprev_words = keep.tile([P, 2 * 2 * T], U8, align_bytes=64)
+        eprev_scales = keep.tile([P, 2 * T], U8, align_bytes=64)
         r_words = keep.tile([P, N], U32, align_bytes=64)
         r_scales = keep.tile([P, N], U8, align_bytes=64)
-        loss_rows = keep.tile([P, P], BF16)
-        loss_rows32 = keep.tile([P, P], F32)
-        loss_cols = keep.tile([P, TILES + N // P], F32)
+        vector_rows = keep.tile([P, P], BF16)
+        vector_rows32 = keep.tile([P, P], F32)
+        vector_cols = keep.tile([P, TILES + CHARGE_ROWS], F32)
         charge_all = keep.tile([P, N], F32)
-        warm = keep.tile([P, 8], F32)
-        scales_early = keep.tile([P, GROUPS * EARLY_SCALE_TILES * P], U8, align_bytes=64)
-        scales_late = keep.tile([P, GROUPS * (TILES - EARLY_SCALE_TILES) * P], U8, align_bytes=64)
+        exp_probe = keep.tile([P, 8], F32)
+        y_scales_early = keep.tile([P, Y_GROUPS * EARLY_SCALE_TILES * P], U8, align_bytes=64)
+        y_scales_late = keep.tile([P, Y_GROUPS * (TILES - EARLY_SCALE_TILES) * P], U8, align_bytes=64)
 
-        x_now, x_prev, base, grouped, x_codes, x_scales = {}, {}, {}, {}, {}, {}
-        y_banks, x_sorted = {}, {}
-        growth, load_bf, y32, y_bf, y_grouped, y_words = {}, {}, {}, {}, {}, {}
+        x_now, x_prev, x_sorted, base = {}, {}, {}, {}
+        turned, codes, scales = {}, {}, {}
+        growth, load_bf = {}, {}
+        y_banks, y32, y_pairs, y_turned, y_words = {}, {}, {}, {}, {}
+
+        def live(i):
+            return 0 <= i < TILES
 
         def rows(i):
             return slice(i * P, (i + 1) * P)
+
+        def group_cols(g):
+            return slice(g * GROUP, (g + 1) * GROUP)
+
 
         def load_prices(i):
             x_now[i] = loads.tile([P, T], BF16, name="x_now")
@@ -80,87 +102,93 @@ def tile_cross_period_demand_settlement_k6_kernel(
                 )
 
         def store_scale_rows(queues, plane, first, count):
+            cols = slice(first * P, (first + count) * P)
             for q in range(4):
                 queues[q % len(queues)].dma_start(
-                    out=out_2[:, 4 * q : 4 * q + 4, first * P : (first + count) * P].bitcast(I32).rearrange("g r m -> r g m"),
-                    in_=plane[32 * q : 32 * q + 4, :].bitcast(I32).rearrange("r (g m) -> r g m", g=GROUPS),
+                    out=out_2[:, 4 * q : 4 * q + 4, cols].bitcast(I32).rearrange("g r m -> r g m"),
+                    in_=plane[32 * q : 32 * q + 4, :].bitcast(I32).rearrange("r (g m) -> r g m", g=Y_GROUPS),
                 )
 
-        def copy_words(dst_words, bank, passes):
+
+        def turn_group(bank, half, pairs_of):
+            for u in range(2):
+                at = (2 * half + u) * P
+                nc.tensor.transpose(bank[:, at : at + P], pairs_of(u), ident[:])
+
+        def copy_turned(dst, src, groups):
             nc.scalar.copy(
-                out=dst_words.rearrange("p (g r u) -> p g r u", g=passes, u=2),
-                in_=bank[:, : passes * 256].rearrange("p (g u r) -> p g r u", g=passes, u=2),
+                out=dst.rearrange("p (g r u) -> p g r u", g=groups, u=2),
+                in_=src.rearrange("p (g u r) -> p g r u", g=groups, u=2),
             )
 
-        def sort_words(i, g, engine):
-            source = x_now[i][:].bitcast(F32) if g == 0 else x_prev[i][:].bitcast(F32)[:, (g - 1) * 256 : g * 256]
-            x_sorted[i, g] = ring.tile([P, 256], F32, name="x_sorted%d" % g, bufs=4)
-            dst = x_sorted[i, g][:].rearrange("m (u p) -> m u p", u=2)
-            src = source.rearrange("m (p u) -> m u p", u=2)
-            if engine == "scalar":
-                nc.scalar.copy(out=dst, in_=src)
-            else:
-                nc.vector.tensor_copy(out=dst, in_=src)
-
-        def price_words(i, g, u):
-            if (i, g) in x_sorted:
-                return x_sorted[i, g][:, u * P : (u + 1) * P]
+        def price_group(i, g):
             if g == 0:
-                return x_now[i][:].bitcast(F32)[:, u:256:2]
-            return x_prev[i][:].bitcast(F32)[:, (g - 1) * 256 + u : g * 256 : 2]
+                return x_now[i][:].bitcast(F32)
+            return x_prev[i][:].bitcast(F32)[:, (g - 1) * PAIRS : g * PAIRS]
+
+        def sort_prices(i):
+            x_sorted[i] = ring.tile([P, PAIRS], F32, name="x_sorted", bufs=SORT_AHEAD + 2)
+            nc.scalar.copy(
+                out=x_sorted[i][:].rearrange("m (u c j) -> m c u j", u=2, j=4),
+                in_=price_group(i, SORTED_GROUP).rearrange("m (c j u) -> m c u j", u=2, j=4),
+            )
+
+        def price_pairs(i, g):
+            if g == SORTED_GROUP and i in x_sorted:
+                return lambda u: x_sorted[i][:, u * P : (u + 1) * P]
+            return lambda u: price_group(i, g)[:, u:PAIRS:2]
 
         def turn_front(s):
-            grouped[s] = ring.tile([P, 4 * 256], F32, name="grouped", align_bytes=64)
-            bank_b = psum.tile([P, KP], F32, name="bank_b")
-            if s < TILES:
-                bank_a = psum.tile([P, KP], F32, name="bank_a")
-                for u in range(2):
-                    nc.tensor.transpose(bank_a[:, u * P : (u + 1) * P], price_words(s, 0, u), ident[:])
-                for u in range(2):
-                    nc.tensor.transpose(bank_a[:, (2 + u) * P : (3 + u) * P], price_words(s, 1, u), ident[:])
-                for u in range(2):
-                    nc.tensor.transpose(bank_b[:, u * P : (u + 1) * P], price_words(s, 2, u), ident[:])
-            if s >= 3:
-                words = load_bf[s - 3][:].bitcast(F32)
-                for u in range(2):
-                    nc.tensor.transpose(bank_b[:, (2 + u) * P : (3 + u) * P], words[:, u * P : (u + 1) * P], ident[:])
-            if s < TILES:
-                copy_words(grouped[s][:, 0:512], bank_a, 2)
-            if s < 3:
-                copy_words(grouped[s][:, 512:768], bank_b, 1)
-            elif s < TILES:
-                copy_words(grouped[s][:, 512:1024], bank_b, 2)
-            else:
-                copy_words(grouped[s][:, 768:1024], bank_b[:, 256:512], 1)
+            turned[s] = ring.tile([P, 4 * PAIRS], F32, name="turned", align_bytes=64)
+            has_prices, has_load = live(s), live(s - LAG_LOAD)
+            bank_b = psum.tile([P, GROUP], F32, name="bank_b")
+            if has_prices:
+                bank_a = psum.tile([P, GROUP], F32, name="bank_a")
+                turn_group(bank_a, 0, price_pairs(s, 0))
+                turn_group(bank_a, 1, price_pairs(s, 1))
+                turn_group(bank_b, 0, price_pairs(s, 2))
+            if has_load:
+                load_pairs = load_bf[s - LAG_LOAD][:].bitcast(F32)
+                turn_group(bank_b, 1, lambda u: load_pairs[:, u * P : (u + 1) * P])
+            if has_prices:
+                copy_turned(turned[s][:, 0 : 2 * PAIRS], bank_a[:], 2)
+            half_from = 0 if has_prices else 1
+            half_to = 2 if has_load else 1
+            copy_turned(
+                turned[s][:, (2 + half_from) * PAIRS : (2 + half_to) * PAIRS],
+                bank_b[:, half_from * PAIRS : half_to * PAIRS],
+                half_to - half_from,
+            )
 
         def quantise_front(s):
-            x_codes[s] = ring.tile([P, 4 * P], U32, name="x_codes", align_bytes=64)
-            x_scales[s] = ring.tile([P, 4 * P], U8, name="x_scales", align_bytes=64)
-            if s < 3:
+            codes[s] = ring.tile([P, 4 * P], U32, name="codes", align_bytes=64)
+            scales[s] = ring.tile([P, 4 * P], U8, name="scales", align_bytes=64)
+            if not live(s - LAG_LOAD):
                 spans = [(0, 2), (2, 3)]
-            elif s < TILES:
+            elif live(s):
                 spans = [(0, 4)]
             else:
                 spans = [(3, 4)]
             for a, b in spans:
                 nc.vector.quantize_mx(
-                    out=x_codes[s][:, a * P : b * P].bitcast(FP8X4),
-                    scales=x_scales[s][:, a * P : b * P],
-                    in_=grouped[s][:, a * 256 : b * 256].bitcast(BF16),
+                    out=codes[s][:, a * P : b * P].bitcast(FP8X4),
+                    scales=scales[s][:, a * P : b * P],
+                    in_=turned[s][:, a * PAIRS : b * PAIRS].bitcast(BF16),
                 )
 
+
         def response(i):
-            bank_z = psum.tile([P, KP], F32, name="bank_z")
+            bank_z = psum.tile([P, GROUP], F32, name="bank_z")
             for g in (1, 2, 0):
                 if g == 0:
-                    rhs, rhs_scale = en_codes[:].bitcast(FP8X4), en_scales[:]
+                    rhs, rhs_scale = elast_codes[:].bitcast(FP8X4), elast_scales[:]
                 else:
-                    rhs = ep_words[:, (g - 1) * 2 * T : g * 2 * T].bitcast(FP4X4)
-                    rhs_scale = ep_scales[:, (g - 1) * T : g * T]
+                    rhs = eprev_words[:, (g - 1) * 2 * T : g * 2 * T].bitcast(FP4X4)
+                    rhs_scale = eprev_scales[:, (g - 1) * T : g * T]
                 nc.tensor.matmul_mx(
                     out=bank_z[:],
-                    lhsT=x_codes[i][:, g * P : (g + 1) * P].bitcast(FP8X4),
-                    lhsT_scale=x_scales[i][:, g * P : (g + 1) * P],
+                    lhsT=codes[i][:, g * P : (g + 1) * P].bitcast(FP8X4),
+                    lhsT_scale=scales[i][:, g * P : (g + 1) * P],
                     rhs=rhs,
                     rhs_scale=rhs_scale,
                     start=(g == 1),
@@ -182,113 +210,143 @@ def tile_cross_period_demand_settlement_k6_kernel(
                 op=ALU.mult,
             )
 
+
         def settle(i):
-            y32[i] = results.tile([P, N], F32, name="y32")
-            banks = []
-            for g in range(GROUPS):
-                bank_y = psum.tile([P, KP], F32, name="bank_y%d" % g)
-                banks.append(bank_y)
+            s = i + LAG_LOAD
+            y_banks[i] = []
+            for g in range(Y_GROUPS):
+                bank_y = psum.tile([P, GROUP], F32, name="bank_y%d" % g)
+                y_banks[i].append(bank_y)
                 nc.tensor.matmul_mx(
                     out=bank_y[:],
-                    lhsT=x_codes[i + 3][:, 3 * P : 4 * P].bitcast(FP8X4),
-                    lhsT_scale=x_scales[i + 3][:, 3 * P : 4 * P],
-                    rhs=r_words[:, g * KP : (g + 1) * KP].bitcast(FP8X4),
-                    rhs_scale=r_scales[:, g * KP : (g + 1) * KP],
+                    lhsT=codes[s][:, 3 * P : 4 * P].bitcast(FP8X4),
+                    lhsT_scale=scales[s][:, 3 * P : 4 * P],
+                    rhs=r_words[:, group_cols(g)].bitcast(FP8X4),
+                    rhs_scale=r_scales[:, group_cols(g)],
                     start=True,
                     stop=True,
                 )
-            y_banks[i] = banks
 
         def finish_y(i):
-            banks = y_banks[i]
-            last = i >= 12
-            for g in range(GROUPS):
+            y32[i] = results.tile([P, N], F32, name="y32")
+            split = i >= FIRST_SPLIT_STORE
+            for g in range(Y_GROUPS):
                 nc.vector.scalar_tensor_tensor(
-                    out=y32[i][:, g * KP : (g + 1) * KP],
-                    in0=banks[g][:],
-                    scalar=loss_cols[:, i : i + 1],
-                    in1=charge_all[:, g * KP : (g + 1) * KP],
+                    out=y32[i][:, group_cols(g)],
+                    in0=y_banks[i][g][:],
+                    scalar=vector_cols[:, i : i + 1],
+                    in1=charge_all[:, group_cols(g)],
                     op0=ALU.mult,
                     op1=ALU.add,
                 )
-                if last:
-                    cols = slice(g * KP, (g + 1) * KP)
-                    nc.sync.dma_start(out=out_0[rows(i), cols], in_=y32[i][:, cols])
-            if not last:
+                if split:
+                    nc.sync.dma_start(out=out_0[rows(i), group_cols(g)], in_=y32[i][:, group_cols(g)])
+            if not split:
                 nc.sync.dma_start(out=out_0[rows(i), :], in_=y32[i][:])
 
-        def round_y(i, g, engine):
-            y_bf[i, g] = ring.tile([P, KP], BF16, name="y_bf%d" % g)
-            dst = y_bf[i, g][:].rearrange("m (u p e) -> m u p e", u=2, e=2)
-            src = y32[i][:, g * KP : (g + 1) * KP].rearrange("m (p u e) -> m u p e", u=2, e=2)
-            if engine == "scalar":
+
+        def round_on_vector(i, first, count):
+            rounded = ring.tile([P, count * GROUP], BF16, name="rounded_vector")
+            nc.vector.tensor_copy(
+                out=rounded[:].rearrange("m (u c j e) -> m c u j e", u=2, j=4, e=2),
+                in_=y32[i][:, first * GROUP : (first + count) * GROUP].rearrange(
+                    "m (c j u e) -> m c u j e", u=2, j=4, e=2
+                ),
+            )
+            pairs = rounded[:].bitcast(F32)
+            for n in range(count):
+                y_pairs[i, first + n] = [pairs[:, (u * count + n) * P : (u * count + n + 1) * P] for u in range(2)]
+
+        def round_elsewhere(i, g, on_scalar):
+            rounded = ring.tile([P, GROUP], BF16, name="rounded%d" % g)
+            dst = rounded[:].rearrange("m (u p e) -> m u p e", u=2, e=2)
+            src = y32[i][:, group_cols(g)].rearrange("m (p u e) -> m u p e", u=2, e=2)
+            if on_scalar:
                 nc.scalar.copy(out=dst, in_=src)
-            elif engine == "vector":
-                nc.vector.tensor_copy(out=dst, in_=src)
             else:
                 nc.gpsimd.tensor_scalar(out=dst, in0=src, scalar1=1.0, scalar2=0.0, op0=ALU.mult, op1=ALU.add)
+            pairs = rounded[:].bitcast(F32)
+            y_pairs[i, g] = [pairs[:, u * P : (u + 1) * P] for u in range(2)]
 
-        def round_y_pair(i):
-            pair_bf = ring.tile([P, 2 * KP], BF16, name="y_bf_pair")
-            y_bf[i, 0], y_bf[i, 1] = pair_bf[:, 0:KP], pair_bf[:, KP : 2 * KP]
-            nc.vector.tensor_copy(
-                out=pair_bf[:].rearrange("m (g u p e) -> m g u p e", g=2, u=2, e=2),
-                in_=y32[i][:, 0 : 2 * KP].rearrange("m (g p u e) -> m g u p e", g=2, u=2, e=2),
-            )
+        def round_on_scalar(i, g):
+            round_elsewhere(i, g, True)
 
-        def turn_y(i, first="bank_c", second="bank_d"):
-            bank_c = psum.tile([P, KP], F32, name=first)
-            bank_d = psum.tile([P, KP], F32, name=second)
-            for g in range(GROUPS):
-                words = y_bf[i, g][:].bitcast(F32)
-                bank = bank_c if g < 2 else bank_d
-                for u in range(2):
-                    at = (2 * (g % 2) + u) * P
-                    nc.tensor.transpose(bank[:, at : at + P], words[:, u * P : (u + 1) * P], ident[:])
-            y_grouped[i] = ring.tile([P, GROUPS * 256], F32, name="y_grouped", tag="handover", align_bytes=64)
-            copy_words(y_grouped[i][:, 0:512], bank_c, 2)
-            copy_words(y_grouped[i][:, 512:768], bank_d, 1)
+        def round_on_gpsimd(i, g):
+            round_elsewhere(i, g, False)
+
+        def turn_y(i, bank_names=("bank_c", "bank_d")):
+            bank_first = psum.tile([P, GROUP], F32, name=bank_names[0])
+            bank_second = psum.tile([P, GROUP], F32, name=bank_names[1])
+            turn_group(bank_first, 0, lambda u: y_pairs[i, 0][u])
+            turn_group(bank_first, 1, lambda u: y_pairs[i, 1][u])
+            turn_group(bank_second, 0, lambda u: y_pairs[i, 2][u])
+            y_turned[i] = ring.tile([P, Y_GROUPS * PAIRS], F32, name="y_turned", tag="handover", align_bytes=64)
+            copy_turned(y_turned[i][:, 0 : 2 * PAIRS], bank_first[:], 2)
+            copy_turned(y_turned[i][:, 2 * PAIRS : 3 * PAIRS], bank_second[:, 0:PAIRS], 1)
 
         def quantise_y(i):
-            width = PAIR
-            j = i % width
-            pair = i - j
+            j = i % WORD_TILES
+            first = i - j
             if j == 0:
-                y_words[pair] = ring.tile([P, GROUPS * width * P], U32, name="y_words", align_bytes=64)
+                y_words[first] = ring.tile([P, Y_GROUPS * WORD_TILES * P], U32, name="y_words", align_bytes=64)
             if i < EARLY_SCALE_TILES:
-                plane, at, count = scales_early, i, EARLY_SCALE_TILES
+                plane, at, count = y_scales_early, i, EARLY_SCALE_TILES
             else:
-                plane, at, count = scales_late, i - EARLY_SCALE_TILES, TILES - EARLY_SCALE_TILES
-            for g in range(GROUPS):
+                plane, at, count = y_scales_late, i - EARLY_SCALE_TILES, TILES - EARLY_SCALE_TILES
+            for g in range(Y_GROUPS):
                 nc.vector.quantize_mx(
-                    out=y_words[pair][:, (g * width + j) * P : (g * width + j + 1) * P].bitcast(FP8X4),
+                    out=y_words[first][:, (g * WORD_TILES + j) * P : (g * WORD_TILES + j + 1) * P].bitcast(FP8X4),
                     scales=plane[:, (g * count + at) * P : (g * count + at + 1) * P],
-                    in_=y_grouped[i][:, g * 256 : (g + 1) * 256].bitcast(BF16),
+                    in_=y_turned[i][:, g * PAIRS : (g + 1) * PAIRS].bitcast(BF16),
                 )
-            if j == width - 1:
+            if j == WORD_TILES - 1:
                 words_out = out_1.rearrange("g p m t -> p g (m t)")
                 nc.sync.dma_start(
-                    out=words_out[:, :, pair * P * 4 : (pair + width) * P * 4].bitcast(I32),
-                    in_=y_words[pair][:].bitcast(I32).rearrange("p (g m) -> p g m", g=GROUPS),
+                    out=words_out[:, :, first * P * 4 : (first + WORD_TILES) * P * 4].bitcast(I32),
+                    in_=y_words[first][:].bitcast(I32).rearrange("p (g m) -> p g m", g=Y_GROUPS),
                 )
             if i == EARLY_SCALE_TILES - 1:
-                store_scale_rows([nc.sync], scales_early, 0, EARLY_SCALE_TILES)
+                store_scale_rows([nc.sync], y_scales_early, 0, EARLY_SCALE_TILES)
             if i == TILES - 1:
-                store_scale_rows([nc.scalar, nc.sync], scales_late, EARLY_SCALE_TILES, TILES - EARLY_SCALE_TILES)
+                store_scale_rows([nc.scalar, nc.sync], y_scales_late, EARLY_SCALE_TILES, TILES - EARLY_SCALE_TILES)
 
-        nc.vector.memset(loss_rows[:], 0.0)
-        nc.vector.memset(ep_scales[:].bitcast(I32), 0)
-        nc.vector.memset(warm[:], 0.0)
-        nc.scalar.activation(out=warm[:, 4:5], in_=warm[:, 0:1], func=ACT.Exp)
+
+        def quantise_elasticities():
+            dst = elast_grouped[:].rearrange("p (c i j) -> p c j i", i=4, j=4)
+            src = elast_raw[:].rearrange("p (j c i) -> p c j i", j=4, i=4)
+            nc.vector.tensor_copy(out=dst[:, 0:ELAST_ON_VECTOR], in_=src[:, 0:ELAST_ON_VECTOR])
+            nc.scalar.copy(out=dst[:, ELAST_ON_VECTOR:P], in_=src[:, ELAST_ON_VECTOR:P])
+            nc.vector.quantize_mx(out=elast_codes[:].bitcast(FP8X4), scales=elast_scales[:], in_=elast_grouped[:])
+
+        def turn_vectors():
+            nc.scalar.copy(out=vector_rows32[:], in_=vector_rows[:])
+            bank_vectors = psum.tile([P, GROUP], F32, name="bank_c")
+            nc.tensor.transpose(bank_vectors[:, 0:P], vector_rows32[:], ident[:])
+            nc.scalar.copy(out=vector_cols[:], in_=bank_vectors[:, 0 : TILES + CHARGE_ROWS])
+
+        def spread_charge():
+            for g in range(Y_GROUPS):
+                bank_charge = psum.tile([P, GROUP], F32, name="bank_y%d" % g)
+                for c in range(4):
+                    col = TILES + 4 * g + c
+                    nc.tensor.transpose(
+                        bank_charge[:, c * P : (c + 1) * P], vector_cols[:, col : col + 1].to_broadcast([P, P]), ident[:]
+                    )
+                nc.vector.tensor_copy(out=charge_all[:, group_cols(g)], in_=bank_charge[:])
+
+        nc.vector.memset(vector_rows[:], 0.0)
+        nc.vector.memset(eprev_scales[:].bitcast(I32), 0)
+        nc.vector.memset(exp_probe[:], 0.0)
+        nc.scalar.activation(out=exp_probe[:, 4:5], in_=exp_probe[:, 0:1], func=ACT.Exp)
         nc.vector.memset(r_scales[:].bitcast(I32), 0)
         make_identity(nc, ident[:])
         load_prices(0)
-        nc.sync.dma_start(out=loss_rows[0:TILES, :], in_=loss.rearrange("(i p) -> i p", p=P))
-        nc.sync.dma_start(out=loss_rows[TILES : TILES + N // P, :], in_=charge.rearrange("(c p) -> c p", p=P))
-        nc.sync.dma_start(out=en_raw[:], in_=elast_now.rearrange("(p j) n -> p (j n)", j=4))
-        load_scale_rows(nc.sync, ep_scales, elast_prev_scales)
+        nc.sync.dma_start(out=vector_rows[0:TILES, :], in_=loss.rearrange("(i p) -> i p", p=P))
+        nc.sync.dma_start(out=vector_rows[TILES : TILES + CHARGE_ROWS, :], in_=charge.rearrange("(c p) -> c p", p=P))
+        nc.sync.dma_start(out=elast_raw[:], in_=elast_now.rearrange("(p j) n -> p (j n)", j=4))
+        load_scale_rows(nc.sync, eprev_scales, elast_prev_scales)
         nc.sync.dma_start(
-            out=ep_words[:].bitcast(I32).rearrange("p (g n) -> p g n", g=2),
+            out=eprev_words[:].bitcast(I32).rearrange("p (g n) -> p g n", g=2),
             in_=elast_prev_words.bitcast(I32).rearrange("g p n -> p g n"),
         )
         load_scale_rows(nc.gpsimd, r_scales, rate_scales)
@@ -303,98 +361,72 @@ def tile_cross_period_demand_settlement_k6_kernel(
         load_prices(4)
         load_baseline(1)
 
-        def quantise_elasticities():
-            dst = en_grouped[:].rearrange("p (c i j) -> p c j i", i=4, j=4)
-            src = en_raw[:].rearrange("p (j c i) -> p c j i", j=4, i=4)
-            nc.vector.tensor_copy(out=dst[:, 0:88], in_=src[:, 0:88])
-            nc.scalar.copy(out=dst[:, 88:128], in_=src[:, 88:128])
-            nc.vector.quantize_mx(out=en_codes[:].bitcast(FP8X4), scales=en_scales[:], in_=en_grouped[:])
-
-        def live(i):
-            return 0 <= i < TILES
-
-        def spread_loss():
-            nc.scalar.copy(out=loss_rows32[:], in_=loss_rows[:])
-            bank_loss = psum.tile([P, KP], F32, name="bank_c")
-            nc.tensor.transpose(bank_loss[:, 0:P], loss_rows32[:], ident[:])
-            nc.scalar.copy(out=loss_cols[:], in_=bank_loss[:, 0 : TILES + N // P])
-
-        def spread_charge():
-            for g in range(GROUPS):
-                bank_charge = psum.tile([P, KP], F32, name="bank_y%d" % g)
-                for c in range(4):
-                    col = TILES + 4 * g + c
-                    nc.tensor.transpose(
-                        bank_charge[:, c * P : (c + 1) * P], loss_cols[:, col : col + 1].to_broadcast([P, P]), ident[:]
-                    )
-                nc.vector.tensor_copy(out=charge_all[:, g * KP : (g + 1) * KP], in_=bank_charge[:])
-
-        spread_loss()
+        turn_vectors()
         turn_front(0)
         quantise_front(0)
         quantise_elasticities()
         spread_charge()
-        sort_words(2, 0, "vector")
-        sort_words(2, 1, "scalar")
+        sort_prices(SORT_AHEAD)
+
         for s in range(1, TILES + 1):
-            if live(s + AHEAD):
-                load_prices(s + AHEAD)
+            if live(s + LOAD_AHEAD):
+                load_prices(s + LOAD_AHEAD)
             if live(s + 1):
                 load_baseline(s + 1)
-            if live(s - 5):
-                round_y_pair(s - 5)
-            if live(s + 2):
-                sort_words(s + 2, 0, "vector")
-            if s < TILES + 3:
-                turn_front(s)
-            if live(s - 6):
-                turn_y(s - 6)
-            if s < TILES + 3:
-                quantise_front(s)
-            if live(s - 7):
-                quantise_y(s - 7)
-            if live(s - 1):
-                response(s - 1)
-            if live(s - 1):
-                responded_load(s - 1)
-            if live(s - 5):
-                round_y(s - 5, 2, "scalar")
-            if live(s + 2):
-                sort_words(s + 2, 1, "scalar")
-            if live(s - 4):
-                settle(s - 4)
-            if live(s - 4):
-                finish_y(s - 4)
-        round_y(12, 0, "scalar")
-        turn_front(17)
-        round_y(12, 1, "scalar")
-        quantise_front(17)
-        quantise_y(10)
-        round_y(12, 2, "gpsimd")
-        turn_y(11)
-        settle(13)
-        finish_y(13)
-        turn_front(18)
-        round_y(13, 0, "gpsimd")
-        quantise_front(18)
-        quantise_y(11)
-        turn_y(12, "bank_a", "bank_z")
-        round_y(13, 1, "scalar")
-        round_y(13, 2, "scalar")
-        quantise_y(12)
-        settle(14)
-        finish_y(14)
-        turn_y(13)
-        round_y(14, 0, "gpsimd")
-        round_y(14, 1, "gpsimd")
-        settle(15)
-        round_y(14, 2, "scalar")
-        finish_y(15)
-        round_y(15, 0, "gpsimd")
-        round_y(15, 1, "scalar")
-        quantise_y(13)
-        turn_y(14, "bank_a", "bank_z")
-        round_y(15, 2, "vector")
-        turn_y(15)
-        quantise_y(14)
-        quantise_y(15)
+            if live(s - LAG_ROUND):
+                round_on_vector(s - LAG_ROUND, 0, 2)
+            turn_front(s)
+            if live(s - LAG_TURN_Y):
+                turn_y(s - LAG_TURN_Y)
+            quantise_front(s)
+            if live(s - LAG_PLANES):
+                quantise_y(s - LAG_PLANES)
+            response(s - LAG_Z)
+            responded_load(s - LAG_Z)
+            if live(s - LAG_ROUND):
+                round_on_scalar(s - LAG_ROUND, 2)
+            if live(s + SORT_AHEAD):
+                sort_prices(s + SORT_AHEAD)
+            if live(s - LAG_Y):
+                settle(s - LAG_Y)
+                finish_y(s - LAG_Y)
+
+        free_banks = ("bank_a", "bank_z")
+        last = TILES - 1
+
+        round_on_scalar(last - 3, 0)
+        turn_front(last - 1 + LAG_LOAD)
+        round_on_scalar(last - 3, 1)
+        quantise_front(last - 1 + LAG_LOAD)
+        quantise_y(last - 5)
+        round_on_scalar(last - 3, 2)
+        turn_y(last - 4)
+        settle(last - 2)
+        finish_y(last - 2)
+
+        turn_front(last + LAG_LOAD)
+        round_on_gpsimd(last - 2, 0)
+        quantise_front(last + LAG_LOAD)
+        quantise_y(last - 4)
+        turn_y(last - 3, free_banks)
+        round_on_scalar(last - 2, 1)
+        round_on_scalar(last - 2, 2)
+        quantise_y(last - 3)
+        settle(last - 1)
+        finish_y(last - 1)
+
+        turn_y(last - 2)
+        round_on_gpsimd(last - 1, 0)
+        round_on_gpsimd(last - 1, 1)
+        settle(last)
+        round_on_scalar(last - 1, 2)
+        finish_y(last)
+
+        round_on_gpsimd(last, 0)
+        round_on_scalar(last, 1)
+        quantise_y(last - 2)
+        turn_y(last - 1, free_banks)
+        round_on_vector(last, 2, 1)
+        turn_y(last)
+        quantise_y(last - 1)
+        quantise_y(last)

@@ -30,12 +30,10 @@ LAG_ROUND = 5
 LAG_TURN_Y = 6
 LAG_PLANES = 7
 LOAD_AHEAD = 4
-SORT_AHEAD = 2
 
-SORTED_GROUP = 1
-ELAST_ON_VECTOR = 88
+ROUND_ON_VECTOR = 46
 WORD_TILES = 2
-EARLY_SCALE_TILES = 10
+EARLY_SCALE_TILES = 8
 FIRST_SPLIT_STORE = 12
 
 
@@ -65,14 +63,13 @@ def tile_cross_period_demand_settlement_k6_kernel(
         vector_rows32 = keep.tile([P, P], F32)
         vector_cols = keep.tile([P, TILES + CHARGE_ROWS], F32)
         charge_all = keep.tile([P, N], F32)
-        exp_probe = keep.tile([P, 8], F32)
         y_scales_early = keep.tile([P, Y_GROUPS * EARLY_SCALE_TILES * P], U8, align_bytes=64)
         y_scales_late = keep.tile([P, Y_GROUPS * (TILES - EARLY_SCALE_TILES) * P], U8, align_bytes=64)
 
-        x_now, x_prev, x_sorted, base = {}, {}, {}, {}
+        x_now, x_prev, base = {}, {}, {}
         turned, codes, scales = {}, {}, {}
         growth, load_bf = {}, {}
-        y_banks, y32, y_pairs, y_turned, y_words = {}, {}, {}, {}, {}
+        y_banks, y32, y_rounded, y_pairs, y_turned, y_words = {}, {}, {}, {}, {}, {}
 
         def live(i):
             return 0 <= i < TILES
@@ -126,16 +123,7 @@ def tile_cross_period_demand_settlement_k6_kernel(
                 return x_now[i][:].bitcast(F32)
             return x_prev[i][:].bitcast(F32)[:, (g - 1) * PAIRS : g * PAIRS]
 
-        def sort_prices(i):
-            x_sorted[i] = ring.tile([P, PAIRS], F32, name="x_sorted", bufs=SORT_AHEAD + 2)
-            nc.scalar.copy(
-                out=x_sorted[i][:].rearrange("m (u c j) -> m c u j", u=2, j=4),
-                in_=price_group(i, SORTED_GROUP).rearrange("m (c j u) -> m c u j", u=2, j=4),
-            )
-
         def price_pairs(i, g):
-            if g == SORTED_GROUP and i in x_sorted:
-                return lambda u: x_sorted[i][:, u * P : (u + 1) * P]
             return lambda u: price_group(i, g)[:, u:PAIRS:2]
 
         def turn_front(s):
@@ -245,34 +233,47 @@ def tile_cross_period_demand_settlement_k6_kernel(
                 nc.sync.dma_start(out=out_0[rows(i), :], in_=y32[i][:])
 
 
-        def round_on_vector(i, first, count):
-            rounded = ring.tile([P, count * GROUP], BF16, name="rounded_vector")
-            nc.vector.tensor_copy(
-                out=rounded[:].rearrange("m (u c j e) -> m c u j e", u=2, j=4, e=2),
-                in_=y32[i][:, first * GROUP : (first + count) * GROUP].rearrange(
-                    "m (c j u e) -> m c u j e", u=2, j=4, e=2
-                ),
+        def line_walk(rounded, values):
+            return (
+                rounded.rearrange("m (u c j e) -> m c u j e", u=2, j=4, e=2),
+                values.rearrange("m (c j u e) -> m c u j e", u=2, j=4, e=2),
             )
-            pairs = rounded[:].bitcast(F32)
-            for n in range(count):
-                y_pairs[i, first + n] = [pairs[:, (u * count + n) * P : (u * count + n + 1) * P] for u in range(2)]
 
-        def round_elsewhere(i, g, on_scalar):
+        def round_vector_share(i):
+            y_rounded[i] = ring.tile([P, N], BF16, name="rounded_all")
+            pairs = y_rounded[i][:].bitcast(F32)
+            for g in range(Y_GROUPS):
+                y_pairs[i, g] = [pairs[:, (u * Y_GROUPS + g) * P : (u * Y_GROUPS + g + 1) * P] for u in range(2)]
+            dst, src = line_walk(y_rounded[i][:], y32[i][:])
+            nc.vector.tensor_copy(out=dst[:, 0:ROUND_ON_VECTOR], in_=src[:, 0:ROUND_ON_VECTOR])
+
+        def round_scalar_share(i):
+            dst, src = line_walk(y_rounded[i][:], y32[i][:])
+            nc.scalar.copy(out=dst[:, ROUND_ON_VECTOR:], in_=src[:, ROUND_ON_VECTOR:])
+
+        def group_tile(i, g):
             rounded = ring.tile([P, GROUP], BF16, name="rounded%d" % g)
-            dst = rounded[:].rearrange("m (u p e) -> m u p e", u=2, e=2)
-            src = y32[i][:, group_cols(g)].rearrange("m (p u e) -> m u p e", u=2, e=2)
-            if on_scalar:
-                nc.scalar.copy(out=dst, in_=src)
-            else:
-                nc.gpsimd.tensor_scalar(out=dst, in0=src, scalar1=1.0, scalar2=0.0, op0=ALU.mult, op1=ALU.add)
             pairs = rounded[:].bitcast(F32)
             y_pairs[i, g] = [pairs[:, u * P : (u + 1) * P] for u in range(2)]
+            return rounded[:]
+
+        def sorted_views(rounded, values):
+            return (
+                rounded.rearrange("m (u p e) -> m u p e", u=2, e=2),
+                values.rearrange("m (p u e) -> m u p e", u=2, e=2),
+            )
+
+        def round_on_vector(i, g):
+            dst, src = line_walk(group_tile(i, g), y32[i][:, group_cols(g)])
+            nc.vector.tensor_copy(out=dst, in_=src)
 
         def round_on_scalar(i, g):
-            round_elsewhere(i, g, True)
+            dst, src = sorted_views(group_tile(i, g), y32[i][:, group_cols(g)])
+            nc.scalar.copy(out=dst, in_=src)
 
         def round_on_gpsimd(i, g):
-            round_elsewhere(i, g, False)
+            dst, src = sorted_views(group_tile(i, g), y32[i][:, group_cols(g)])
+            nc.gpsimd.tensor_scalar(out=dst, in0=src, scalar1=1.0, scalar2=0.0, op0=ALU.mult, op1=ALU.add)
 
         def turn_y(i, bank_names=("bank_c", "bank_d")):
             bank_first = psum.tile([P, GROUP], F32, name=bank_names[0])
@@ -311,15 +312,7 @@ def tile_cross_period_demand_settlement_k6_kernel(
                 store_scale_rows([nc.scalar, nc.sync], y_scales_late, EARLY_SCALE_TILES, TILES - EARLY_SCALE_TILES)
 
 
-        def quantise_elasticities():
-            dst = elast_grouped[:].rearrange("p (c i j) -> p c j i", i=4, j=4)
-            src = elast_raw[:].rearrange("p (j c i) -> p c j i", j=4, i=4)
-            nc.vector.tensor_copy(out=dst[:, 0:ELAST_ON_VECTOR], in_=src[:, 0:ELAST_ON_VECTOR])
-            nc.scalar.copy(out=dst[:, ELAST_ON_VECTOR:P], in_=src[:, ELAST_ON_VECTOR:P])
-            nc.vector.quantize_mx(out=elast_codes[:].bitcast(FP8X4), scales=elast_scales[:], in_=elast_grouped[:])
-
         def turn_vectors():
-            nc.scalar.copy(out=vector_rows32[:], in_=vector_rows[:])
             bank_vectors = psum.tile([P, GROUP], F32, name="bank_c")
             nc.tensor.transpose(bank_vectors[:, 0:P], vector_rows32[:], ident[:])
             nc.scalar.copy(out=vector_cols[:], in_=bank_vectors[:, 0 : TILES + CHARGE_ROWS])
@@ -336,8 +329,6 @@ def tile_cross_period_demand_settlement_k6_kernel(
 
         nc.vector.memset(vector_rows[:], 0.0)
         nc.vector.memset(eprev_scales[:].bitcast(I32), 0)
-        nc.vector.memset(exp_probe[:], 0.0)
-        nc.scalar.activation(out=exp_probe[:, 4:5], in_=exp_probe[:, 0:1], func=ACT.Exp)
         nc.vector.memset(r_scales[:].bitcast(I32), 0)
         make_identity(nc, ident[:])
         load_prices(0)
@@ -361,12 +352,16 @@ def tile_cross_period_demand_settlement_k6_kernel(
         load_prices(4)
         load_baseline(1)
 
-        turn_vectors()
+        nc.scalar.activation(out=vector_rows32[:], in_=vector_rows[:], func=ACT.Copy)
         turn_front(0)
+        turn_vectors()
+        nc.vector.tensor_copy(
+            out=elast_grouped[:].rearrange("p (c i j) -> p c j i", i=4, j=4),
+            in_=elast_raw[:].rearrange("p (j c i) -> p c j i", j=4, i=4),
+        )
         quantise_front(0)
-        quantise_elasticities()
+        nc.vector.quantize_mx(out=elast_codes[:].bitcast(FP8X4), scales=elast_scales[:], in_=elast_grouped[:])
         spread_charge()
-        sort_prices(SORT_AHEAD)
 
         for s in range(1, TILES + 1):
             if live(s + LOAD_AHEAD):
@@ -374,19 +369,17 @@ def tile_cross_period_demand_settlement_k6_kernel(
             if live(s + 1):
                 load_baseline(s + 1)
             if live(s - LAG_ROUND):
-                round_on_vector(s - LAG_ROUND, 0, 2)
+                round_vector_share(s - LAG_ROUND)
             turn_front(s)
-            if live(s - LAG_TURN_Y):
-                turn_y(s - LAG_TURN_Y)
             quantise_front(s)
             if live(s - LAG_PLANES):
                 quantise_y(s - LAG_PLANES)
             response(s - LAG_Z)
+            if live(s - LAG_TURN_Y):
+                turn_y(s - LAG_TURN_Y)
             responded_load(s - LAG_Z)
             if live(s - LAG_ROUND):
-                round_on_scalar(s - LAG_ROUND, 2)
-            if live(s + SORT_AHEAD):
-                sort_prices(s + SORT_AHEAD)
+                round_scalar_share(s - LAG_ROUND)
             if live(s - LAG_Y):
                 settle(s - LAG_Y)
                 finish_y(s - LAG_Y)
@@ -426,7 +419,7 @@ def tile_cross_period_demand_settlement_k6_kernel(
         round_on_scalar(last, 1)
         quantise_y(last - 2)
         turn_y(last - 1, free_banks)
-        round_on_vector(last, 2, 1)
+        round_on_vector(last, 2)
         turn_y(last)
         quantise_y(last - 1)
         quantise_y(last)

from contextlib import ExitStack

import concourse.mybir as mybir
from concourse.masks import make_identity

M, T, PREV, N = 2048, 512, 1024, 1536
FLOPS = 2 * M * T * (T + PREV) + 2 * M * T * N

F32 = mybir.dt.float32
BF16 = mybir.dt.bfloat16
U32 = mybir.dt.uint32
I32 = mybir.dt.int32
U8 = mybir.dt.uint8
FP8X4 = mybir.dt.float8_e4m3fn_x4
FP4X4 = mybir.dt.float4_e2m1fn_x4
ACT = mybir.ActivationFunctionType
ALU = mybir.AluOpType

P = 128
GROUP = 512
PAIRS = GROUP // 2
TILES = M // P
Y_GROUPS = N // GROUP
CHARGE_ROWS = N // P

LAG_Z = 1
LAG_LOAD = 3
LAG_Y = 4
LAG_ROUND = 5
LAG_TURN_Y = 6
LAG_PLANES = 7
LOAD_AHEAD = 4

ROUND_ON_VECTOR = 46
WORD_TILES = 2
EARLY_SCALE_TILES = 8
FIRST_SPLIT_STORE = 12


def tile_cross_period_demand_settlement_k6_kernel(
    tc, dlog_now, dlog_prev, elast_now, elast_prev_words, elast_prev_scales, baseline,
    rate_words, rate_scales, loss, charge, out_0, out_1, out_2,
):
    nc = tc.nc
    with ExitStack() as ctx:
        keep = ctx.enter_context(tc.tile_pool(name="keep", bufs=1))
        ring = ctx.enter_context(tc.tile_pool(name="ring", bufs=3))
        loads = ctx.enter_context(tc.tile_pool(name="loads", bufs=LOAD_AHEAD + 3))
        results = ctx.enter_context(tc.tile_pool(name="results", bufs=5))
        psum = ctx.enter_context(tc.psum_pool(name="psum", bufs=1))
        ctx.enter_context(tc.manual_schedule())

        ident = keep.tile([P, P], F32)
        elast_raw = keep.tile([P, 4 * T], BF16, align_bytes=64)
        elast_grouped = keep.tile([P, 4 * T], BF16, align_bytes=64)
        elast_codes = keep.tile([P, T], U32, align_bytes=64)
        elast_scales = keep.tile([P, T], U8, align_bytes=64)
        eprev_words = keep.tile([P, 2 * 2 * T], U8, align_bytes=64)
        eprev_scales = keep.tile([P, 2 * T], U8, align_bytes=64)
        r_words = keep.tile([P, N], U32, align_bytes=64)
        r_scales = keep.tile([P, N], U8, align_bytes=64)
        vector_rows = keep.tile([P, P], BF16)
        vector_rows32 = keep.tile([P, P], F32)
        vector_cols = keep.tile([P, TILES + CHARGE_ROWS], F32)
        charge_all = keep.tile([P, N], F32)
        y_scales_early = keep.tile([P, Y_GROUPS * EARLY_SCALE_TILES * P], U8, align_bytes=64)
        y_scales_late = keep.tile([P, Y_GROUPS * (TILES - EARLY_SCALE_TILES) * P], U8, align_bytes=64)

        x_now, x_prev, base = {}, {}, {}
        turned, codes, scales = {}, {}, {}
        growth, load_bf = {}, {}
        y_banks, y32, y_rounded, y_pairs, y_turned, y_words = {}, {}, {}, {}, {}, {}

        def live(i):
            return 0 <= i < TILES

        def rows(i):
            return slice(i * P, (i + 1) * P)

        def group_cols(g):
            return slice(g * GROUP, (g + 1) * GROUP)


        def load_prices(i):
            x_now[i] = loads.tile([P, T], BF16, name="x_now")
            x_prev[i] = loads.tile([P, PREV], BF16, name="x_prev")
            nc.sync.dma_start(out=x_now[i][:], in_=dlog_now[rows(i), :])
            nc.sync.dma_start(out=x_prev[i][:], in_=dlog_prev[rows(i), :])

        def load_baseline(i):
            base[i] = loads.tile([P, T], BF16, name="base")
            nc.sync.dma_start(out=base[i][:], in_=baseline[rows(i), :])

        def load_scale_rows(queue, plane, src):
            for q in range(4):
                queue.dma_start(
                    out=plane[32 * q : 32 * q + 4, :].bitcast(I32).rearrange("r (g n) -> r g n", g=src.shape[0]),
                    in_=src[:, 4 * q : 4 * q + 4, :].bitcast(I32).rearrange("g r n -> r g n"),
                )

        def store_scale_rows(queues, plane, first, count):
            cols = slice(first * P, (first + count) * P)
            for q in range(4):
                queues[q % len(queues)].dma_start(
                    out=out_2[:, 4 * q : 4 * q + 4, cols].bitcast(I32).rearrange("g r m -> r g m"),
                    in_=plane[32 * q : 32 * q + 4, :].bitcast(I32).rearrange("r (g m) -> r g m", g=Y_GROUPS),
                )


        def turn_group(bank, half, pairs_of):
            for u in range(2):
                at = (2 * half + u) * P
                nc.tensor.transpose(bank[:, at : at + P], pairs_of(u), ident[:])

        def copy_turned(dst, src, groups):
            nc.scalar.copy(
                out=dst.rearrange("p (g r u) -> p g r u", g=groups, u=2),
                in_=src.rearrange("p (g u r) -> p g r u", g=groups, u=2),
            )

        def price_group(i, g):
            if g == 0:
                return x_now[i][:].bitcast(F32)
            return x_prev[i][:].bitcast(F32)[:, (g - 1) * PAIRS : g * PAIRS]

        def price_pairs(i, g):
            return lambda u: price_group(i, g)[:, u:PAIRS:2]

        def turn_front(s):
            turned[s] = ring.tile([P, 4 * PAIRS], F32, name="turned", align_bytes=64)
            has_prices, has_load = live(s), live(s - LAG_LOAD)
            bank_b = psum.tile([P, GROUP], F32, name="bank_b")
            if has_prices:
                bank_a = psum.tile([P, GROUP], F32, name="bank_a")
                turn_group(bank_a, 0, price_pairs(s, 0))
                turn_group(bank_a, 1, price_pairs(s, 1))
                turn_group(bank_b, 0, price_pairs(s, 2))
            if has_load:
                load_pairs = load_bf[s - LAG_LOAD][:].bitcast(F32)
                turn_group(bank_b, 1, lambda u: load_pairs[:, u * P : (u + 1) * P])
            if has_prices:
                copy_turned(turned[s][:, 0 : 2 * PAIRS], bank_a[:], 2)
            half_from = 0 if has_prices else 1
            half_to = 2 if has_load else 1
            copy_turned(
                turned[s][:, (2 + half_from) * PAIRS : (2 + half_to) * PAIRS],
                bank_b[:, half_from * PAIRS : half_to * PAIRS],
                half_to - half_from,
            )

        def quantise_front(s):
            codes[s] = ring.tile([P, 4 * P], U32, name="codes", align_bytes=64)
            scales[s] = ring.tile([P, 4 * P], U8, name="scales", align_bytes=64)
            if not live(s - LAG_LOAD):
                spans = [(0, 2), (2, 3)]
            elif live(s):
                spans = [(0, 4)]
            else:
                spans = [(3, 4)]
            for a, b in spans:
                nc.vector.quantize_mx(
                    out=codes[s][:, a * P : b * P].bitcast(FP8X4),
                    scales=scales[s][:, a * P : b * P],
                    in_=turned[s][:, a * PAIRS : b * PAIRS].bitcast(BF16),
                )


        def response(i):
            bank_z = psum.tile([P, GROUP], F32, name="bank_z")
            for g in (1, 2, 0):
                if g == 0:
                    rhs, rhs_scale = elast_codes[:].bitcast(FP8X4), elast_scales[:]
                else:
                    rhs = eprev_words[:, (g - 1) * 2 * T : g * 2 * T].bitcast(FP4X4)
                    rhs_scale = eprev_scales[:, (g - 1) * T : g * T]
                nc.tensor.matmul_mx(
                    out=bank_z[:],
                    lhsT=codes[i][:, g * P : (g + 1) * P].bitcast(FP8X4),
                    lhsT_scale=scales[i][:, g * P : (g + 1) * P],
                    rhs=rhs,
                    rhs_scale=rhs_scale,
                    start=(g == 1),
                    stop=(g == 0),
                )
            growth[i] = ring.tile([P, T], F32, name="growth")
            nc.scalar.activation(
                out=growth[i][:].rearrange("m (u p e) -> m u p e", u=2, e=2),
                in_=bank_z[:].rearrange("m (p u e) -> m u p e", u=2, e=2),
                func=ACT.Exp,
            )

        def responded_load(i):
            load_bf[i] = ring.tile([P, T], BF16, name="load_bf", tag="handover", align_bytes=64)
            nc.gpsimd.tensor_tensor(
                out=load_bf[i][:].rearrange("m (u p e) -> m u p e", u=2, e=2),
                in0=growth[i][:].rearrange("m (u p e) -> m u p e", u=2, e=2),
                in1=base[i][:].rearrange("m (p u e) -> m u p e", u=2, e=2),
                op=ALU.mult,
            )


        def settle(i):
            s = i + LAG_LOAD
            y_banks[i] = []
            for g in range(Y_GROUPS):
                bank_y = psum.tile([P, GROUP], F32, name="bank_y%d" % g)
                y_banks[i].append(bank_y)
                nc.tensor.matmul_mx(
                    out=bank_y[:],
                    lhsT=codes[s][:, 3 * P : 4 * P].bitcast(FP8X4),
                    lhsT_scale=scales[s][:, 3 * P : 4 * P],
                    rhs=r_words[:, group_cols(g)].bitcast(FP8X4),
                    rhs_scale=r_scales[:, group_cols(g)],
                    start=True,
                    stop=True,
                )

        def finish_y(i):
            y32[i] = results.tile([P, N], F32, name="y32")
            split = i >= FIRST_SPLIT_STORE
            for g in range(Y_GROUPS):
                nc.vector.scalar_tensor_tensor(
                    out=y32[i][:, group_cols(g)],
                    in0=y_banks[i][g][:],
                    scalar=vector_cols[:, i : i + 1],
                    in1=charge_all[:, group_cols(g)],
                    op0=ALU.mult,
                    op1=ALU.add,
                )
                if split:
                    nc.sync.dma_start(out=out_0[rows(i), group_cols(g)], in_=y32[i][:, group_cols(g)])
            if not split:
                nc.sync.dma_start(out=out_0[rows(i), :], in_=y32[i][:])


        def line_walk(rounded, values):
            return (
                rounded.rearrange("m (u c j e) -> m c u j e", u=2, j=4, e=2),
                values.rearrange("m (c j u e) -> m c u j e", u=2, j=4, e=2),
            )

        def round_vector_share(i):
            y_rounded[i] = ring.tile([P, N], BF16, name="rounded_all")
            pairs = y_rounded[i][:].bitcast(F32)
            for g in range(Y_GROUPS):
                y_pairs[i, g] = [pairs[:, (u * Y_GROUPS + g) * P : (u * Y_GROUPS + g + 1) * P] for u in range(2)]
            dst, src = line_walk(y_rounded[i][:], y32[i][:])
            nc.vector.tensor_copy(out=dst[:, 0:ROUND_ON_VECTOR], in_=src[:, 0:ROUND_ON_VECTOR])

        def round_scalar_share(i):
            dst, src = line_walk(y_rounded[i][:], y32[i][:])
            nc.scalar.copy(out=dst[:, ROUND_ON_VECTOR:], in_=src[:, ROUND_ON_VECTOR:])

        def group_tile(i, g):
            rounded = ring.tile([P, GROUP], BF16, name="rounded%d" % g)
            pairs = rounded[:].bitcast(F32)
            y_pairs[i, g] = [pairs[:, u * P : (u + 1) * P] for u in range(2)]
            return rounded[:]

        def sorted_views(rounded, values):
            return (
                rounded.rearrange("m (u p e) -> m u p e", u=2, e=2),
                values.rearrange("m (p u e) -> m u p e", u=2, e=2),
            )

        def round_on_vector(i, g):
            dst, src = line_walk(group_tile(i, g), y32[i][:, group_cols(g)])
            nc.vector.tensor_copy(out=dst, in_=src)

        def round_on_scalar(i, g):
            dst, src = sorted_views(group_tile(i, g), y32[i][:, group_cols(g)])
            nc.scalar.copy(out=dst, in_=src)

        def round_on_gpsimd(i, g):
            dst, src = sorted_views(group_tile(i, g), y32[i][:, group_cols(g)])
            nc.gpsimd.tensor_scalar(out=dst, in0=src, scalar1=1.0, scalar2=0.0, op0=ALU.mult, op1=ALU.add)

        def turn_y(i, bank_names=("bank_c", "bank_d")):
            bank_first = psum.tile([P, GROUP], F32, name=bank_names[0])
            bank_second = psum.tile([P, GROUP], F32, name=bank_names[1])
            turn_group(bank_first, 0, lambda u: y_pairs[i, 0][u])
            turn_group(bank_first, 1, lambda u: y_pairs[i, 1][u])
            turn_group(bank_second, 0, lambda u: y_pairs[i, 2][u])
            y_turned[i] = ring.tile([P, Y_GROUPS * PAIRS], F32, name="y_turned", tag="handover", align_bytes=64)
            copy_turned(y_turned[i][:, 0 : 2 * PAIRS], bank_first[:], 2)
            copy_turned(y_turned[i][:, 2 * PAIRS : 3 * PAIRS], bank_second[:, 0:PAIRS], 1)

        def quantise_y(i):
            j = i % WORD_TILES
            first = i - j
            if j == 0:
                y_words[first] = ring.tile([P, Y_GROUPS * WORD_TILES * P], U32, name="y_words", align_bytes=64)
            if i < EARLY_SCALE_TILES:
                plane, at, count = y_scales_early, i, EARLY_SCALE_TILES
            else:
                plane, at, count = y_scales_late, i - EARLY_SCALE_TILES, TILES - EARLY_SCALE_TILES
            for g in range(Y_GROUPS):
                nc.vector.quantize_mx(
                    out=y_words[first][:, (g * WORD_TILES + j) * P : (g * WORD_TILES + j + 1) * P].bitcast(FP8X4),
                    scales=plane[:, (g * count + at) * P : (g * count + at + 1) * P],
                    in_=y_turned[i][:, g * PAIRS : (g + 1) * PAIRS].bitcast(BF16),
                )
            if j == WORD_TILES - 1:
                words_out = out_1.rearrange("g p m t -> p g (m t)")
                nc.sync.dma_start(
                    out=words_out[:, :, first * P * 4 : (first + WORD_TILES) * P * 4].bitcast(I32),
                    in_=y_words[first][:].bitcast(I32).rearrange("p (g m) -> p g m", g=Y_GROUPS),
                )
            if i == EARLY_SCALE_TILES - 1:
                store_scale_rows([nc.sync], y_scales_early, 0, EARLY_SCALE_TILES)
            if i == TILES - 1:
                store_scale_rows([nc.scalar, nc.sync], y_scales_late, EARLY_SCALE_TILES, TILES - EARLY_SCALE_TILES)


        def turn_vectors():
            bank_vectors = psum.tile([P, GROUP], F32, name="bank_c")
            nc.tensor.transpose(bank_vectors[:, 0:P], vector_rows32[:], ident[:])
            nc.scalar.copy(out=vector_cols[:], in_=bank_vectors[:, 0 : TILES + CHARGE_ROWS])

        def spread_charge():
            for g in range(Y_GROUPS):
                bank_charge = psum.tile([P, GROUP], F32, name="bank_y%d" % g)
                for c in range(4):
                    col = TILES + 4 * g + c
                    nc.tensor.transpose(
                        bank_charge[:, c * P : (c + 1) * P], vector_cols[:, col : col + 1].to_broadcast([P, P]), ident[:]
                    )
                nc.vector.tensor_copy(out=charge_all[:, group_cols(g)], in_=bank_charge[:])

        nc.vector.memset(vector_rows[:], 0.0)
        nc.vector.memset(eprev_scales[:].bitcast(I32), 0)
        nc.vector.memset(r_scales[:].bitcast(I32), 0)
        make_identity(nc, ident[:])
        load_prices(0)
        nc.sync.dma_start(out=vector_rows[0:TILES, :], in_=loss.rearrange("(i p) -> i p", p=P))
        nc.sync.dma_start(out=vector_rows[TILES : TILES + CHARGE_ROWS, :], in_=charge.rearrange("(c p) -> c p", p=P))
        nc.sync.dma_start(out=elast_raw[:], in_=elast_now.rearrange("(p j) n -> p (j n)", j=4))
        load_scale_rows(nc.sync, eprev_scales, elast_prev_scales)
        nc.sync.dma_start(
            out=eprev_words[:].bitcast(I32).rearrange("p (g n) -> p g n", g=2),
            in_=elast_prev_words.bitcast(I32).rearrange("g p n -> p g n"),
        )
        load_scale_rows(nc.gpsimd, r_scales, rate_scales)
        load_prices(1)
        load_prices(2)
        load_baseline(0)
        load_prices(3)
        nc.sync.dma_start(
            out=r_words[:].bitcast(I32),
            in_=rate_words[0].rearrange("p n t -> p (n t)").bitcast(I32),
        )
        load_prices(4)
        load_baseline(1)

        nc.scalar.activation(out=vector_rows32[:], in_=vector_rows[:], func=ACT.Copy)
        turn_front(0)
        turn_vectors()
        nc.vector.tensor_copy(
            out=elast_grouped[:].rearrange("p (c i j) -> p c j i", i=4, j=4),
            in_=elast_raw[:].rearrange("p (j c i) -> p c j i", j=4, i=4),
        )
        quantise_front(0)
        nc.vector.quantize_mx(out=elast_codes[:].bitcast(FP8X4), scales=elast_scales[:], in_=elast_grouped[:])
        spread_charge()

        for s in range(1, TILES + 1):
            if live(s + LOAD_AHEAD):
                load_prices(s + LOAD_AHEAD)
            if live(s + 1):
                load_baseline(s + 1)
            if live(s - LAG_ROUND):
                round_vector_share(s - LAG_ROUND)
            turn_front(s)
            quantise_front(s)
            if live(s - LAG_PLANES):
                quantise_y(s - LAG_PLANES)
            response(s - LAG_Z)
            if live(s - LAG_TURN_Y):
                turn_y(s - LAG_TURN_Y)
            responded_load(s - LAG_Z)
            if live(s - LAG_ROUND):
                round_scalar_share(s - LAG_ROUND)
            if live(s - LAG_Y):
                settle(s - LAG_Y)
                finish_y(s - LAG_Y)

        free_banks = ("bank_a", "bank_z")
        last = TILES - 1

        round_on_scalar(last - 3, 0)
        turn_front(last - 1 + LAG_LOAD)
        round_on_scalar(last - 3, 1)
        quantise_front(last - 1 + LAG_LOAD)
        quantise_y(last - 5)
        round_on_scalar(last - 3, 2)
        turn_y(last - 4)
        settle(last - 2)
        finish_y(last - 2)

        turn_front(last + LAG_LOAD)
        round_on_gpsimd(last - 2, 0)
        quantise_front(last + LAG_LOAD)
        quantise_y(last - 4)
        turn_y(last - 3, free_banks)
        round_on_scalar(last - 2, 1)
        round_on_scalar(last - 2, 2)
        quantise_y(last - 3)
        settle(last - 1)
        finish_y(last - 1)

        turn_y(last - 2)
        round_on_gpsimd(last - 1, 0)
        round_on_gpsimd(last - 1, 1)
        settle(last)
        round_on_scalar(last - 1, 2)
        finish_y(last)

        round_on_gpsimd(last, 0)
        round_on_scalar(last, 1)
        quantise_y(last - 2)
        turn_y(last - 1, free_banks)
        round_on_vector(last, 2)
        turn_y(last)
        quantise_y(last - 1)
        quantise_y(last)
